import numpy as np, ml_dtypes
CORES = [25,29,65,69,153,157,193,197]
N = 8
BF = ml_dtypes.bfloat16
C, L, B, S, P, VOTE = 1024, 256, 2, 5, 8, 64
R = B * L
M = N * R
def parts(rng):
    z = rng.integers(0, 256, (N, 8, 16, C)) + rng.integers(-64, 65, (N, 8, 1, C))
    return {"cd": rng.integers(0, 16, (N, 8, 16, C)), "zt": np.clip(z, 0, 255), "kid": rng.integers(0, C, (N, 8, C)), "ky": rng.integers(0, C, (N, 8, C)),
            "e0": rng.integers(0, M, (N, 8, 16, L)), "c0": rng.integers(0, C, (N, 8, L)), "x0": rng.integers(0, 256, (N, 8, 16, R)),
            "ce0": rng.integers(0, M, (N, 8, 16, R)), "cc0": rng.integers(0, C, (N, 8, R))}
def pack(d):
    o = {}
    for k in ("cd", "zt", "kid", "ky", "e0", "c0", "x0", "ce0", "cc0"):
        v = np.ascontiguousarray(d[k].reshape(N, -1, d[k].shape[-1]))
        o[k] = v.astype(np.float32).astype(BF) if k in ("zt", "x0") else v.astype(np.int32)
    return o
def setup_inputs(rng):
    return pack(parts(rng))
def uneven(rng, n, shape, coin):
    v = np.minimum(np.exp2(rng.random(shape) * np.log2(n + 1.0)).astype(np.int64) - 1, n - 1)
    return np.where(rng.random(coin) < 0.5, v, n - 1 - v)
def setup_inputs_spread(rng):
    return pack({"cd": uneven(rng, 16, (N, 8, 16, C), (N, 8, 1, C)), "zt": uneven(rng, 256, (N, 8, 16, C), (N, 8, 1, C)),
                 "kid": uneven(rng, C, (N, 8, C), (N, 8, C)), "ky": uneven(rng, C, (N, 8, C), (N, 8, C)),
                 "e0": uneven(rng, M, (N, 8, 16, L), (N, 8, 1, L)), "c0": uneven(rng, C, (N, 8, L), (N, 8, L)),
                 "x0": uneven(rng, 256, (N, 8, 16, R), (N, 8, 1, R)), "ce0": uneven(rng, M, (N, 8, 16, R), (N, 8, 1, R)), "cc0": uneven(rng, C, (N, 8, R), (N, 8, R))})
def mix(rng, hi, *shape):
    v = np.where(rng.random(shape) < 0.5, 0, hi)
    return np.where(rng.random(shape) < 0.72, v, rng.integers(0, hi + 1, shape))
def setup_inputs_ends(rng):
    d = {"cd": mix(rng, 15, N, 8, 16, C), "zt": mix(rng, 255, N, 8, 16, C), "kid": mix(rng, C - 1, N, 8, C), "ky": mix(rng, C - 1, N, 8, C),
         "e0": mix(rng, M - 1, N, 8, 16, L), "c0": mix(rng, C - 1, N, 8, L), "x0": mix(rng, 255, N, 8, 16, R), "ce0": mix(rng, M - 1, N, 8, 16, R), "cc0": mix(rng, C - 1, N, 8, R)}
    rec = rng.random((N, 8, 1, R)); d["x0"] = np.where(rec < 0.15, 0, np.where(rec < 0.3, 255, d["x0"]))
    d["e0"][:, :, 0] = np.where(rng.random((N, 8, L)) < 0.8, rng.integers(0, M, (N, 8, L)), d["e0"][:, :, 0])
    d["ce0"][:, :, 0] = np.where(rng.random((N, 8, R)) < 0.8, rng.integers(0, M, (N, 8, R)), d["ce0"][:, :, 0])
    d["cd"][:, :, 0] = np.where(rng.random((N, 8, C)) < 0.7, 0, d["cd"][:, :, 0])
    d["x0"][0, :, :, 0] = 0; d["x0"][N - 1, :, :, R - 1] = 255
    cd, zt, c0 = d["cd"], d["zt"], d["c0"]
    cd[:, :, :8, C - 1] = 0; cd[:, :, 8:, C - 1] = 15
    cd[:, :, :, 0] = 0; cd[:, :, 15, 0] = 15
    cd[:, :, :, C - 2] = 0
    zt[..., 0] = np.where(rng.random((N, 8, 16)) < 0.5, 255, 0); zt[..., C - 2] = 255
    for q in range(N):
        v = np.full(128, 255); v[rng.permutation(128)[:VOTE - q % 2]] = 0; zt[q, :, :, C - 1] = v.reshape(8, 16)
    c0[..., 0] = C - 1; c0[..., L - 1] = C - 1; c0[..., 1] = 0; c0[..., L - 2] = 0; c0[..., 2] = C - 2; c0[..., L - 3] = C - 2
    for i in (0, 1, 2, L - 3, L - 2, L - 1): d["e0"][:, :, 0, i] = 0; d["e0"][:, :, 15, i] = M - 1
    return pack(d)
def setup_inputs_corners(rng):
    d = parts(rng); own = lambda n, top, *lead: 16 * rng.integers(0, top // 16, lead + (n,)) + np.arange(n) % 16
    d["kid"] = own(C, C, N, 8); d["ky"] = own(C, C, N, 8); d["e0"] = own(L, M, N, 8, 16); d["c0"] = own(L, C, N, 8); d["ce0"] = own(R, M, N, 8, 16); d["cc0"] = own(R, C, N, 8)
    d["x0"] = 2 * rng.integers(0, 128, (N, 8, 16, R)); d["e0"][:, :, 0, 0] = 0; d["e0"][:, :, 15, L - 1] = M - 1; d["c0"][..., 0] = 0; d["c0"][..., L - 1] = C - 1
    want = (0, 1, 2, 3, VOTE - 16, VOTE - 2, VOTE - 1, VOTE - 1, VOTE, VOTE, VOTE + 1, VOTE + 16, 112, 126, 127, 128)
    need = np.zeros((N, 8, 16), np.int64)
    for q in range(N):
        for k in range(16): need[q, :, k] = np.bincount(rng.permutation(128)[:want[(k + 5 * q) % 16]] // 16, minlength=8)
    place = np.argsort(np.argsort(rng.random((N, 8, 16, C)), axis=2), axis=2)
    d["zt"] = np.where(place < need[:, :, np.arange(C) % 16][:, :, None, :], 0, 255)
    return pack(d)
def setup_inputs_crowd(rng):
    d = parts(rng); mode = rng.permutation(8); s = np.arange(R)
    one = rng.choice(np.array([0, M - 1, M // 2, R - 1]), 8); lane = int(rng.integers(0, L))
    for q in range(N):
        for g in range(8):
            m = mode[g]
            if m < 2:
                ke, kc = d["e0"][q, g, :, lane].copy(), d["c0"][q, g, lane]
                d["e0"][q, g] = one[g]; d["c0"][q, g] = (0, C - 1)[q % 2]
                if m == 1: d["e0"][q, g, :, lane] = ke; d["c0"][q, g, lane] = (kc + (kc == 0)) % (C - 1)
            elif m == 2: d["e0"][q, g] = np.where(rng.random((16, L)) < 0.5, 0, M - 1)
            elif m == 3: d["e0"][q, g] = q * R + np.arange(L); d["ce0"][q, g] = q * R + s
            elif m == 4: d["cd"][q, g] = 0
            elif m == 5: d["cd"][q, g] = 15
            elif m == 6: d["ce0"][q, g] = (q * R + s + 1) % M; d["cd"][q, g] = np.arange(16)[:, None]
            else:
                for k in ("c0", "kid", "ky", "cc0"): d[k][q, g] = rng.choice(np.array([0, C - 1, C // 2]), d[k][q, g].shape)
    return pack(d)
def setup_inputs_full(rng):
    d = parts(rng); K = 16 // N; kind = rng.permutation(np.arange(N) % 4)[:, None, None]; o = int(rng.integers(0, N))
    cd = np.argsort(rng.random((N, 8, 16, C)), axis=2); u = (np.arange(N) + int(rng.integers(0, N))).reshape(N, 1, 1, 1)
    cd = (cd + (u - cd[:, :, :1]) % N) % 16
    s = np.argsort(rng.random((N, 8, B, N, R)), axis=4)[..., :K * L].reshape(N, 8, B, N, K, L)
    s = s + R * ((np.arange(8)[:, None] + np.arange(N)[None, :]) % N).reshape(1, 8, 1, N, 1, 1)
    c0 = 2 * np.argsort(rng.random((N, 8, C // 2)), axis=2)[..., :L] + np.where(kind < 2, rng.integers(0, 2, (N, 8, L)), kind - 2)
    kid = np.argsort(rng.random((N, 8, C)), axis=2); kk = kind[..., None]
    e0 = o * R + rng.integers(0, R, (N, 8, 16, L))
    t0 = o * R + L * rng.integers(0, B, (N, 8, 1)) + np.argsort(rng.random((N, 8, L)), axis=2)
    np.put_along_axis(e0, np.take_along_axis(cd[:, :, 0], c0, 2)[:, :, None, :], t0[:, :, None, :], 2)
    d["cd"] = cd; d["ce0"] = s.transpose(0, 1, 4, 3, 2, 5).reshape(N, 8, 16, R); d["c0"] = c0; d["e0"] = e0
    d["kid"] = np.where(kind < 2, kid, kid | 1); d["ky"] = d["ky"] & -2; d["cc0"] = d["cc0"] & -2; d["x0"] = d["x0"] & -2
    z = np.where(kk == 0, 0, np.where(kk == 1, 255, 255 * (np.arange(C) % 2)))
    d["zt"] = np.array(np.broadcast_to(z, (N, 8, 16, C)))
    return pack(d)
def check_inputs(d):
    bad = []
    for k, hi in (("cd", 15), ("zt", 255), ("kid", C - 1), ("ky", C - 1), ("e0", M - 1), ("c0", C - 1), ("x0", 255), ("ce0", M - 1), ("cc0", C - 1)):
        v = np.asarray(d[k]).astype(np.float64)
        if not (np.min(v) >= 0 and np.max(v) <= hi): bad.append("range of " + k)
        elif np.any(v != np.floor(v)): bad.append("whole numbers of " + k)
    return bad
def reference(cd, zt, kid, ky, e0, c0, x0, ce0, cc0):
    row = cd.astype(np.int64).reshape(N, 8, 16, C); z = zt.astype(np.float32).astype(np.int64).reshape(N, 8, 16, C)
    kd = kid.astype(np.int64); kc = ky.astype(np.int64); e = e0.astype(np.int64).reshape(N, 8, 16, L); c = c0.astype(np.int64)
    hx = np.array(x0.astype(np.float32).astype(np.int64).reshape(N, 8, 16, R).transpose(1, 2, 0, 3)).reshape(8, 16, M)
    he = np.array(ce0.astype(np.int64).reshape(N, 8, 16, R).transpose(1, 2, 0, 3)).reshape(8, 16, M)
    hc = np.array(cc0.astype(np.int64).transpose(1, 0, 2)).reshape(8, M)
    out = []
    for t in range(S):
        nm = np.take_along_axis(e, np.take_along_axis(row, c[:, :, None, :], 3), 2)
        w = []
        for q in range(N):
            v = np.take_along_axis(hx, nm[q].reshape(8, 1, 16 * L), 2).reshape(8, 16, 16 // P, P, L)
            w.append(np.add.reduce(np.maximum.reduce(v, axis=2), axis=2) & 255)
        w = np.stack(w)
        yes = (w >= np.take_along_axis(z, c[:, :, None, :], 3)).astype(np.int64)
        binds = np.add.reduce(yes.reshape(N, 128, L), axis=1) >= VOTE
        place = np.arange(N)[:, None] * R + L * (t % B) + np.arange(L)[None, :]
        first = np.broadcast_to(place[:, None, None, :], (N, 8, 1, L))
        eb = np.concatenate([first, e[:, :, :15]], axis=2)
        ea = np.stack([np.take_along_axis(he, nm[q][:, 0:1, :], 2) for q in range(N)])
        ca = np.stack([np.take_along_axis(hc, nm[q][:, 0, :], 1) for q in range(N)])
        en = np.where(binds[:, None, None, :], eb, ea); cn = np.where(binds[:, None, :], np.take_along_axis(kd, c, 2), ca)
        if t < S - 1:
            kq = np.take_along_axis(kc, c, 2)
            for q in range(N):
                lo = q * R + L * (t % B)
                hx[:, :, lo:lo + L] = w[q]; he[:, :, lo:lo + L] = e[q]; hc[:, lo:lo + L] = kq[q]
        e = en; c = cn; out.append(w.reshape(N, 128, L))
    return {"ye": e.reshape(N, 128, L).astype(np.float32), "yc": c.astype(np.float32), "yx": np.concatenate(out, axis=2).astype(np.float32).astype(BF)}

@@ -1,0 +1,418 @@
+from concourse.bass import DstId, RemoteDMATransfer
+from concourse.mybir import AluOpType as ALU, ActivationFunctionType as ACT
+
+STEPS, LANES, BLK, WORLD = 5, 256, 2048, 256
+MATS = ["I", "NI", "SH", "DL", "DH", "UP", "DN", "D0", "M9", "M85", "ROW0", "BD", "ON", "E8"] + ["P%d" % m for m in range(8)]
+
+
+def _sb(n, d):
+    return ("sbuf", [128, n], d)
+
+
+SCRATCH = {
+    "xw": _sb(6 * BLK, "bfloat16"), "ew": _sb(6 * BLK, "float32"),
+    "nmi": _sb(768, "int32"), "nmf": _sb(768, "float32"), "nmh": _sb(768, "bfloat16"), "nmr": _sb(768, "bfloat16"),
+    "c8i": _sb(768, "int32"), "c8h": _sb(768, "float16"),
+    "cdi": _sb(1024, "int32"), "vtab": _sb(1024, "bfloat16"), "stab": _sb(1024, "bfloat16"), "ztab": _sb(1024, "bfloat16"),
+    "kki": _sb(128, "int32"), "kka": _sb(128, "float16"), "kkb": _sb(128, "float16"),
+    "kidt": _sb(1024, "float32"), "kyt": _sb(1024, "float32"),
+    "pci": _sb(4, "int32"), "cols": _sb(32, "float32"), "jm": _sb(128, "bfloat16"), "gm": _sb(128, "bfloat16"),
+    "ge": _sb(128, "bfloat16"), "km": _sb(256, "bfloat16"), "nt": _sb(256, "bfloat16"),
+    "mats": _sb(128 * len(MATS), "bfloat16"), "idf": _sb(128, "float32"),
+    "pa1": _sb(256, "bfloat16"), "pa2": _sb(256, "bfloat16"), "pat": _sb(256, "float32"),
+    "cvote": _sb(256, "bfloat16"), "csum": _sb(256, "bfloat16"),
+    "pw": _sb(256, "float32"), "rr": _sb(256, "float32"), "sc": _sb(256, "float32"), "sc0": _sb(256, "float32"),
+    "l1": _sb(16, "int32"), "l2": _sb(16, "int32"), "ql": _sb(16, "uint16"), "l0": _sb(16, "uint16"),
+    "xh": _sb(256, "float16"), "xf": _sb(256, "float32"), "uu": _sb(256, "bfloat16"), "pen": _sb(2048, "bfloat16"),
+    "acc": _sb(256, "float32"), "yy": _sb(256, "float32"), "ti": _sb(256, "int32"), "tj": _sb(256, "int32"), "ta": _sb(256, "int32"),
+    "zh": _sb(256, "float16"), "ll": _sb(256, "uint16"), "aw": _sb(256, "float32"), "kg": _sb(256, "float32"),
+    "ga": _sb(2048, "bfloat16"), "mx": _sb(2048, "bfloat16"), "xr": _sb(256, "bfloat16"), "w4": _sb(256, "bfloat16"),
+    "yes": _sb(256, "bfloat16"), "v2": _sb(256, "float32"),
+    "hb": _sb(256, "bfloat16"), "bb": _sb(256, "bfloat16"), "oe": _sb(256, "float32"), "oc": _sb(256, "float32"),
+}
+for _b in range(8):
+    SCRATCH["ps%d" % _b] = ("psum", [128, 512], "float32")
+
+MSGS = ["xa", "xb", "ea", "eb"] + [k + str(t) for t in range(STEPS - 1) for k in ("me", "mw")]
+SEMAPHORES = ["sv", "ss", "sp", "sg", "sent", "sto", "lxa", "lxb", "lce", "le", "lc8", "lcd", "lzt", "lkk"] + MSGS
+
+
+def _piece(T, msg, r):
+    blk = {"xa": 0, "xb": 1, "ea": 0, "eb": 1}.get(msg)
+    if blk is None:
+        blk = 2 + int(msg[2:])
+    buf = T.xw if _kind(msg) == 0 else T.ew
+    a = blk * BLK + r * LANES
+    return buf[:, a:a + LANES]
+
+
+def _kind(msg):
+    return 0 if msg[0] == "x" or msg[1] == "w" else 1
+
+
+def _bits(engines):
+    m = 0
+    for e in engines:
+        m |= 1 << e
+    return m
+
+
+def _routes(cores, topo):
+    place = lambda c: (topo.host(c), topo.chip(c))
+    near, used = {}, set()
+    for s in cores:
+        far = [d for d in cores if not topo.may_write(s, d)]
+        near[s] = [c for c in topo.cores_of(s) if c not in cores and topo.die(c) == topo.die(s) and all(topo.may_write(c, d) for d in far)]
+        used.update(near[s])
+    first, hand = ({}, {}), {}
+    for r, s in enumerate(cores):
+        sib = [d for d in cores if d != s and place(d) == place(s)]
+        plane = [d for d in cores if topo.same_plane(s, d)]
+        far = [d for d in cores if not topo.may_write(s, d)]
+        here = [d for d in far if topo.host(d) == topo.host(s)]
+        there = [d for d in far if topo.host(d) != topo.host(s)]
+        mate = [c for c in range(WORLD) if topo.mates(c, there[0]) and topo.die(c) == topo.die(s)
+                and topo.may_write(s, c) and all(topo.may_write(c, d) for d in there)]
+        inner = [c for c in topo.cores_of(plane[0]) if c not in cores and c not in used and topo.die(c) == topo.die(s)]
+        off = topo.engines(s, mate[0])
+        on = [e for e in topo.engines(s, sib[0]) if e not in off]
+        for kind in (0, 1):
+            a, b, c = near[s][kind], mate[kind], inner[0]
+            first[kind][r] = [(b, off[:len(off) // 2]), (c, off[len(off) // 2:]), (a, on[:len(on) // 2]), (sib[0], on[len(on) // 2:])]
+            for relay, dests in ((a, here), (b, there), (c, plane)):
+                en = topo.engines(relay, dests[0])
+                k = len(en) // len(dests)
+                hand.setdefault(relay, []).append((kind, r, [(d, en[i * k:(i + 1) * k]) for i, d in enumerate(dests)]))
+    return first, hand
+
+
+def _send(g, T, topo, core, msg, r, dests):
+    ap = _piece(T, msg, r)
+    tr = []
+    for d, en in dests:
+        rid, pid = topo.addr(d, core)
+        tr.append(RemoteDMATransfer(dst_ids=[DstId(rid=rid, pnc=pid)], dma_engine_mask=_bits(en), remote_sem=T.sem[msg], src=ap, dst=ap))
+    g.remote_dma_fused(tr, local_sem=T.sem.sent)
+    return sum(len(en) for d, en in dests)
+
+
+def rank_program(g, core, T, topo):
+    cores = list(T.cores)
+    first, hand = _routes(cores, topo)
+    rank = T.rank_of(core)
+    if rank is None:
+        sent = 0
+        for msg in MSGS:
+            for kind, r, dests in hand.get(core, []):
+                if kind == _kind(msg):
+                    g.wait_ge(T.sem[msg], sum(len(en) for d, en in first[kind][r] if d == core))
+                    sent += _send(g, T, topo, core, msg, r, dests)
+        if sent:
+            g.wait_ge(T.sem.sent, sent)
+        return
+
+    arrive = [0, 0]
+    for kind in (0, 1):
+        arrive[kind] += sum(len(en) for r in first[kind] for d, en in first[kind][r] if d == core)
+    for relay in hand:
+        for kind, r, dests in hand[relay]:
+            arrive[kind] += sum(len(en) for d, en in dests if d == core)
+
+    Q = {"v": g.vector, "s": g.scalar, "p": g.tensor, "g": g, "y": g.sync}
+    known = {q: {} for q in Q}
+    count = {q: 0 for q in Q}
+    res, bank = {}, {}
+
+    def need(q, events):
+        want = {}
+        for sem, val, clock in events:
+            if known[q].get(sem, 0) < val and want.get(sem, (0, None))[0] < val:
+                want[sem] = (val, clock)
+        for sem in sorted(want, key=lambda s: -len(want[s][1])):
+            val, clock = want[sem]
+            if known[q].get(sem, 0) < val:
+                Q[q].wait_ge(T.sem[sem], val)
+                known[q][sem] = val
+                for k in clock:
+                    known[q][k] = max(known[q].get(k, 0), clock[k])
+
+    def deps(q, r, w, b):
+        ev = []
+        for k in r:
+            ev += res.get(k, ([], []))[0]
+        for k in w:
+            ev += res.get(k, ([], []))[0] + res.get(k, ([], []))[1]
+        for k in b:
+            ev += [e for qq, e in bank.get(k, {}).items() if qq != q]
+        need(q, ev)
+
+    def op(q, fn, r=(), w=(), b=()):
+        deps(q, r, w, b)
+        count[q] += 1
+        fn().then_inc(T.sem["s" + q], 1)
+        e = ("s" + q, count[q], dict(known[q]))
+        for k in r:
+            res.setdefault(k, ([], []))[1].append(e)
+        for k in w:
+            res[k] = ([e], [])
+        for k in b:
+            bank.setdefault(k, {})[q] = e
+
+    def landed(key, sem, val):
+        res[key] = ([(sem, val, {})], [])
+
+    V, S, PE = g.vector, g.scalar, g.tensor
+    ps = [T["ps%d" % i] for i in range(8)]
+
+    def mat(name):
+        i = MATS.index(name)
+        return T.mats[:, 128 * i:128 * (i + 1)]
+
+    def ts(out, in0, s1, s2, o0, o1, r, w, b=()):
+        if o1 is None:
+            op("v", lambda: V.tensor_scalar(out, in0, s1, None, o0), r, w, b)
+        else:
+            op("v", lambda: V.tensor_scalar(out, in0, s1, s2, o0, o1), r, w, b)
+
+    def tt(out, in0, in1, o, r, w, b=()):
+        op("v", lambda: V.tensor_tensor(out, in0, in1, o), r, w, b)
+
+    def cp(out, in0, r, w, b=()):
+        op("v", lambda: V.tensor_copy(out, in0), r, w, b)
+
+    def act(out, in0, f, r, w, b=(), bias=0.0, scale=1.0):
+        op("s", lambda: S.activation(out, in0, f, bias=bias, scale=scale), r, w, b)
+
+    def mm(bk, out, lhs, rhs, start, stop, r):
+        op("p", lambda: PE.matmul(out, lhs, rhs, start, stop), r, (), (bk,))
+
+    sent = [0]
+
+    def send(msg, r):
+        deps("g", r, (), ())
+        sent[0] += _send(g, T, topo, core, msg, rank, first[_kind(msg)][rank])
+
+    g.sync.dma_start(_piece(T, "xa", rank), T.x0[:, 0:256]).then_inc(T.sem.lxa, 16)
+    g.sync.dma_start(_piece(T, "xb", rank), T.x0[:, 256:512]).then_inc(T.sem.lxb, 16)
+    g.scalar.dma_start(T.nmi[:, 0:512], T.ce0[:]).then_inc(T.sem.lce, 16)
+    g.scalar.dma_start(T.nmi[:, 512:768], T.e0[:]).then_inc(T.sem.le, 16)
+    g.scalar.dma_start(T.c8i[0:8, 0:512], T.cc0[:]).then_inc(T.sem.lc8, 16)
+    g.scalar.dma_start(T.c8i[0:8, 512:768], T.c0[:]).then_inc(T.sem.lc8, 16)
+    g.sync.dma_start(T.cdi[:], T.cd[:]).then_inc(T.sem.lcd, 16)
+    g.sync.dma_start(T.kki[:, 0:64], T.kid[:]).then_inc(T.sem.lkk, 16)
+    g.sync.dma_start(T.kki[:, 64:128], T.ky[:]).then_inc(T.sem.lkk, 16)
+    g.sync.dma_start(T.ztab[:], T.zt[:]).then_inc(T.sem.lzt, 16)
+    for key, sem, val in (("own_x0", "lxa", 16), ("own_x1", "lxb", 16), ("nmi0", "lce", 16), ("nmi1", "le", 16), ("c8i", "lc8", 32),
+                          ("cdi", "lcd", 16), ("kki", "lkk", 32), ("ztab", "lzt", 16)):
+        landed(key, sem, val)
+    for msg in MSGS:
+        landed("in_" + msg, msg, arrive[_kind(msg)])
+    xin = ["in_xa", "in_xb"] + ["in_mw%d" % t for t in range(STEPS - 1)]
+    ein = ["in_ea", "in_eb"] + ["in_me%d" % t for t in range(STEPS - 1)]
+
+    op("g", lambda: g.iota(T.pci[:, 0:1], [[0, 1]], 0, 1), (), ("pc",))
+    op("g", lambda: g.iota(T.jm[:], [[1, 128]], 0, -1, allow_small_or_imprecise_dtypes=True), (), ("jm",))
+    op("g", lambda: g.iota(T.gm[:], [[1, 8], [0, 16]], 0, 0, allow_small_or_imprecise_dtypes=True), (), ("gm",))
+    op("g", lambda: g.iota(T.km[:], [[0, 16], [1, 16]], 0, 0, allow_small_or_imprecise_dtypes=True), (), ("km",))
+    send("xa", ["own_x0"])
+    send("xb", ["own_x1"])
+    op("g", lambda: g.iota(T.nt[:], [[1, 256]], 0, 0, allow_small_or_imprecise_dtypes=True), (), ("nt",))
+
+    BIG, C35, EPS = float(2 ** 23), 1.5 * 2.0 ** 35, 2.0 ** -12
+    op("v", lambda: V.memset(mat("ON"), float(2 ** 24)), (), ("ON",))
+    op("v", lambda: V.memset(T.cvote[:], -127.0 / 256), (), ("cvote",))
+    op("v", lambda: V.memset(T.csum[:], 384.0 * 2.0 ** -24), (), ("csum",))
+    CN = ["gg", "pp", "jj", "lo", "hi", "his", "n15", "e0", "e0s", "j1", "a1", "a2", "uc", "cc", "t0a", "t0", "nb0", "nb1"]
+    col = lambda n: T.cols[:, CN.index(n):CN.index(n) + 1]
+    ts(T.pci[:, 1:2], T.pci[:, 0:1], 15, None, ALU.bitwise_and, None, ["pc"], ["pj"])
+    ts(T.pci[:, 2:3], T.pci[:, 0:1], 4, None, ALU.arith_shift_right, None, ["pc"], ["pg"])
+    cp(col("pp"), T.pci[:, 0:1], ["pc"], ["pp"])
+    ts(mat("M9"), T.jm[:], 0.0, -9.0, ALU.is_equal, ALU.mult, ["jm"], ["M9"])
+    ts(mat("M85"), T.jm[:], 0.0, 8.5, ALU.is_equal, ALU.mult, ["jm"], ["M85"])
+    ts(T.idf[:], T.jm[:], 0.0, None, ALU.is_equal, None, ["jm"], ["idf"])
+    jji = T.pci[:, 1:2]
+    cp(col("gg"), T.pci[:, 2:3], ["pg"], ["gg"])
+    cp(col("jj"), jji, ["pj"], ["jj"])
+    ts(col("a1"), jji, -1.0, 7.0, ALU.mult, ALU.add, ["pj"], ["a1"])
+    ts(col("a2"), jji, -8.0, None, ALU.add, None, ["pj"], ["a2"])
+    ts(col("cc"), jji, 8.0, EPS, ALU.is_ge, ALU.max, ["pj"], ["cc"])
+    ts(col("e0s"), jji, 0.0, EPS, ALU.is_equal, ALU.mult, ["pj"], ["e0s"])
+    ts(mat("E8"), T.gm[:], col("pp"), 4096.0, ALU.is_equal, ALU.mult, ["gm", "pp"], ["E8"])
+    ts(mat("BD"), T.gm[:], col("gg"), 4096.0, ALU.is_equal, ALU.mult, ["gm", "gg"], ["BD"])
+    tt(col("uc"), col("a1"), col("a2"), ALU.max, ["a1", "a2"], ["uc"])
+    ts(col("lo"), jji, 8.0, None, ALU.is_lt, None, ["pj"], ["lo"])
+    ts(col("hi"), jji, 8.0, None, ALU.is_ge, None, ["pj"], ["hi"])
+    ts(col("his"), jji, 8.0, EPS, ALU.is_ge, ALU.mult, ["pj"], ["his"])
+    ts(col("j1"), jji, 1.0, None, ALU.add, None, ["pj"], ["j1"])
+    ts(T.cols[:, 24:32], T.km[:, 0:8], col("uc"), col("cc"), ALU.is_equal, ALU.mult, ["km", "uc", "cc"], ["co"])
+    for m in range(8):
+        act(mat("P%d" % m), mat("BD"), ACT.Identity, ["BD", "co"], ["P%d" % m], scale=T.cols[:, 24 + m:25 + m])
+    act(mat("ROW0"), mat("BD"), ACT.Identity, ["BD", "e0s"], ["ROW0"], scale=col("e0s"))
+    ts(T.pa1[:], T.km[:], col("jj"), -4 * BIG, ALU.is_equal, ALU.mult, ["km", "jj"], ["pa1"])
+    ts(T.pa2[:], T.km[:], col("j1"), BIG, ALU.is_equal, ALU.mult, ["km", "j1"], ["pa2"])
+    ts(mat("NI"), T.jm[:], 0.0, -1.0, ALU.is_equal, ALU.mult, ["jm"], ["NI"])
+
+    for k, (a, e) in enumerate(((0, 512), (512, 768))):
+        cp(T.nmf[:, a:e], T.nmi[:, a:e], ["nmi%d" % k], ["nmf%d" % k])
+        ts(T.c8h[0:8, a:e], T.c8i[0:8, a:e], -96.0, None, ALU.add, None, ["c8i"], ["c8h%d" % k])
+        act(T.nmh[:, a:e], T.nmf[:, a:e], ACT.Identity, ["nmf%d" % k], ["nmh%d" % k], bias=49152 - 127.5)
+        act(T.nmr[:, a:e], T.nmf[:, a:e], ACT.Identity, ["nmf%d" % k], ["nmr%d" % k], bias=98304 - 255.5)
+        o = ps[k][:, 0:e - a]
+        i8 = MATS.index("E8") * 128
+        mm(k, o, T.idf[:], T.nmf[:, a:e], True, False, ["idf", "nmf%d" % k])
+        mm(k, o, T.mats[0:8, i8:i8 + 128], T.c8h[0:8, a:e], False, False, ["E8", "c8h%d" % k])
+        mm(k, o, mat("M9"), T.nmh[:, a:e], False, False, ["M9", "nmh%d" % k])
+        mm(k, o, mat("M85"), T.nmr[:, a:e], False, True, ["M85", "nmr%d" % k])
+    act(_piece(T, "ea", rank), ps[0][:, 0:256], ACT.Copy, [], ["own_e0"], (0,))
+    act(_piece(T, "eb", rank), ps[0][:, 256:512], ACT.Copy, [], ["own_e1"], (0,))
+    act(T.pw[:], ps[1][:, 0:256], ACT.Copy, [], ["pw"], (1,))
+    send("ea", ["own_e0"])
+    send("eb", ["own_e1"])
+    tt(T.pat[:], T.pa1[:], T.pa2[:], ALU.add, ["pa1", "pa2"], ["pat"])
+    cp(T.vtab[:], T.cdi[:], ["cdi"], ["vtab"])
+
+    def late_constants():
+        ts(T.kka[:], T.kki[:], col("lo"), None, ALU.mult, None, ["kki", "lo"], ["kka"])
+        ts(T.kkb[:], T.kki[:], col("his"), None, ALU.mult, None, ["kki", "his"], ["kkb"])
+        ts(T.stab[:], T.vtab[:], 8.0, EPS, ALU.is_lt, ALU.max, ["vtab"], ["stab"])
+        ts(col("n15"), jji, 15.0, None, ALU.is_lt, None, ["pj"], ["n15"])
+        ts(col("e0"), jji, 0.0, None, ALU.is_equal, None, ["pj"], ["e0"])
+        ts(col("nb0"), jji, 0.0, float(256 * rank), ALU.is_equal, ALU.mult, ["pj"], ["nb0"])
+        ts(col("nb1"), jji, 0.0, float(256 * rank - 2048), ALU.is_equal, ALU.mult, ["pj"], ["nb1"])
+        ts(mat("DL"), T.jm[:], 0.0, col("lo"), ALU.is_equal, ALU.mult, ["jm", "lo"], ["DL"])
+        ts(mat("DH"), T.jm[:], 0.0, col("hi"), ALU.is_equal, ALU.mult, ["jm", "hi"], ["DH"])
+        ts(mat("UP"), T.jm[:], 8.0, col("lo"), ALU.is_equal, ALU.mult, ["jm", "lo"], ["UP"])
+        ts(mat("DN"), T.jm[:], -8.0, col("hi"), ALU.is_equal, ALU.mult, ["jm", "hi"], ["DN"])
+        ts(mat("I"), T.jm[:], 0.0, None, ALU.is_equal, None, ["jm"], ["I"])
+        ts(col("t0"), col("n15"), -BIG, 2048.0, ALU.mult, ALU.add, ["n15"], ["t0"])
+        ts(mat("SH"), T.jm[:], 1.0, col("n15"), ALU.is_equal, ALU.mult, ["jm", "n15"], ["SH"])
+        ts(mat("D0"), T.jm[:], 0.0, col("e0"), ALU.is_equal, ALU.mult, ["jm", "e0"], ["D0"])
+
+    def code_table(a, banks):
+        for c in range(16):
+            m, src = (7 - c, "kka") if c < 8 else (c - 8, "kkb")
+            bk = banks[c // 8]
+            mm(bk, ps[bk][:, 64 * (c % 8):64 * (c % 8) + 64], mat("P%d" % m), T[src][:, a:a + 64], True, True, ["P%d" % m, src])
+
+    def split(xout, xkey):
+        ts(T.rr[:], T.pw[:], 0.5, C35, ALU.add, ALU.add, ["pw"], ["rr"])
+        act(ps[4][:, 0:256], T.rr[:], ACT.Identity, ["rr"], [], (4,), bias=-C35)
+        return lambda: tt(xout, T.pw[:], ps[4][:, 0:256], ALU.subtract, ["pw"], [xkey], (4,))
+
+    nsto = 0
+    for t in range(STEPS):
+        last = t == STEPS - 1
+        qg = lambda tab: tab[:, 0:1024].indirect(T.ql[:, 0:16])
+        fin = split(T.xh[:], "xh")
+        op("v", lambda: V.tensor_tensor_scan(T.sc[:], T.pat[:], T.pw[:], 0.0, ALU.add, ALU.max), ["pat", "pw"], ["sc"])
+        ts(T.l1[:], T.sc[:, 15:256:16], 2048.0, None, ALU.add, None, ["sc"], ["l1"])
+        ts(T.l2[:], T.l1[:], 12, 1023, ALU.arith_shift_right, ALU.bitwise_and, ["l1"], ["l2"])
+        cp(T.ql[:], T.l2[:], ["l2"], ["ql"])
+        fin()
+        act(T.uu[:], qg(T.vtab), ACT.Abs, ["vtab", "ql"], ["uu"], bias=-7.5)
+
+        def word():
+            if not last:
+                tt(_piece(T, "me%d" % t, rank), qg(T.kyt), T.xh[:], ALU.add, ["kyt", "ql", "xh"], ["own_e%d" % (t + 2)])
+
+        if t == 0:
+            late_constants()
+        else:
+            word()
+        for m in range(8):
+            pm = T.pen[:, 256 * m:256 * (m + 1)]
+            act(pm, T.uu[:], ACT.Abs, ["uu"], ["pen%d" % m], bias=-(m + 0.5) * 2.0 ** 25, scale=2.0 ** 25)
+            bk = m % 4
+            mm(bk, ps[bk][:, 0:256], mat("P%d" % m), T.xh[:], True, False, ["P%d" % m, "xh"])
+            mm(bk, ps[bk][:, 0:256], mat("NI"), pm, False, True, ["NI", "pen%d" % m])
+            if t == 0 and m == 3:
+                code_table(64, (5, 6))
+            if m == 0:
+                cp(T.acc[:], ps[bk][:, 0:256], [], ["acc"], (bk,))
+            else:
+                tt(T.acc[:], ps[bk][:, 0:256], T.acc[:], ALU.max, ["acc"], ["acc"], (bk,))
+        if t == 0:
+            for h in range(2):
+                act(T.kyt[:, 512 * h:512 * h + 512], ps[5 + h][:], ACT.Identity, [], ["kyt%d" % h], (5 + h,), scale=4096.0)
+            res["kyt"] = (res["kyt0"][0] + res["kyt1"][0], [])
+            code_table(0, (0, 1))
+            for h in range(2):
+                act(T.kidt[:, 512 * h:512 * h + 512], ps[h][:], ACT.Identity, [], ["kidt%d" % h], (h,), scale=4096.0, bias=float(2 ** 22))
+            res["kidt"] = (res["kidt0"][0] + res["kidt1"][0], [])
+        nb = "nb%d" % (t % 2)
+        act(T.kg[:], qg(T.kidt), ACT.Identity, ["kidt", "ql", nb], ["kg"], bias=col(nb))
+        tt(T.yy[:], qg(T.stab), T.acc[:], ALU.mult, ["stab", "ql", "acc"], ["yy"])
+        ts(T.ti[:], T.yy[:], 2.0 ** -13, None, ALU.add, None, ["yy"], ["ti"])
+        if t % 2:
+            ts(T.tj[:], T.ti[:], 2048.0, None, ALU.add, None, ["ti"], ["tj"])
+            ts(T.ta[:], T.tj[:], 4095, None, ALU.bitwise_and, None, ["tj"], ["ta"])
+        else:
+            ts(T.ta[:], T.ti[:], 4095, None, ALU.bitwise_and, None, ["ti"], ["ta"])
+        ts(T.zh[:], T.ta[:], -2048.0, None, ALU.add, None, ["ta"], ["zh"])
+        ev, od = T.zh[:, 0:256:2], T.zh[:, 1:256:2]
+        mm(4, ps[4][:, 0:128], mat("DL"), ev, True, False, ["DL", "zh"])
+        mm(4, ps[4][:, 0:128], mat("UP"), od, False, True, ["UP", "zh"])
+        mm(4, ps[4][:, 128:256], mat("DN"), ev, True, False, ["DN", "zh"])
+        mm(4, ps[4][:, 128:256], mat("DH"), od, False, True, ["DH", "zh"])
+        mm(6, ps[6][:, 0:256], mat("ROW0"), T.zh[:], True, True, ["ROW0", "zh"])
+        ts(T.ll[:], ps[4][:, 0:256], 2048.0, None, ALU.add, None, [], ["ll"], (4,))
+        op("v", lambda: V.tensor_tensor_scan(T.sc0[:], T.pat[:], ps[6][:, 0:256], 0.0, ALU.add, ALU.max), ["pat"], ["sc0"], (6,))
+        ts(T.l0[:], T.sc0[:, 15:256:16], col("t0"), None, ALU.add, None, ["sc0", "t0"], ["l0"])
+        if t == 0:
+            word()
+        mm(7, ps[7][:, 0:256], mat("SH"), T.xh[:], True, False, ["SH", "xh"])
+        mm(7, ps[7][:, 0:256], mat("D0"), T.nt[:], False, False, ["D0", "nt"])
+        mm(7, ps[7][:, 0:256], T.idf[:], T.kg[:], False, True, ["idf", "kg"])
+        mm(5, ps[5][:, 0:256], mat("ON"), T.csum[:], True, False, ["ON", "csum"])
+        mm(6, ps[6][:, 0:256], mat("ON"), T.cvote[:], True, False, ["ON", "cvote"])
+
+        have = [xin[t], xin[t + 1], "own_x%d" % t, "own_x%d" % (t + 1)]
+        if not last:
+            send("me%d" % t, have + ["own_e%d" % (t + 2)])
+        win = T.xw[:, BLK * t:BLK * (t + 2)]
+        for c in range(8):
+            a = 256 * c
+            act(T.ga[:, a:a + 256], win.indirect(T.ll[:, 128 + 16 * c:144 + 16 * c]), ACT.Copy, have + ["ll"], ["ga%d" % c])
+            tt(T.mx[:, a:a + 256], win.indirect(T.ll[:, 16 * c:16 * c + 16]), T.ga[:, a:a + 256], ALU.max,
+               have + ["ll", "ga%d" % c], ["mx%d" % c])
+            if c % 2:
+                q = c // 2
+                for k in range(8):
+                    mm(5, ps[5][:, 64 * q:64 * q + 64], mat("I"), T.mx[:, 512 * q + k:512 * q + 512:8], False, q == 3 and k == 7,
+                       ["I", "mx%d" % (c - 1), "mx%d" % c])
+        act(T.xr[:], ps[5][:, 0:256], ACT.Identity, [], ["xr"], (5,), bias=-127.5)
+        wap = T.w4[:] if last else _piece(T, "mw%d" % t, rank)
+        wk = "own_x%d" % (t + 2)
+        tt(wap, ps[5][:, 0:256], T.xr[:], ALU.subtract, ["xr"], [wk], (5,))
+        if not last:
+            send("mw%d" % t, [wk])
+        deps("y", [wk], (), ())
+        g.sync.dma_start(T.yx[:, 256 * t:256 * (t + 1)], wap).then_inc(T.sem.sto, 16)
+        nsto += 16
+        act(T.aw[:], T.ew[:, BLK * t:BLK * (t + 2)].indirect(T.l0[:, 0:16]), ACT.Copy,
+            [ein[t], ein[t + 1], "own_e%d" % t, "own_e%d" % (t + 1), "l0"], ["aw"])
+        tt(T.yes[:], qg(T.ztab), wap, ALU.is_le, ["ztab", "ql", wk], ["yes"])
+        mm(6, ps[6][:, 0:256], mat("ON"), T.yes[:], False, True, ["ON", "yes"])
+        tt(T.v2[:], ps[6][:, 0:256], T.aw[:], ALU.max, ["aw"], ["v2"], (6,))
+        tt(T.pw[:], ps[7][:, 0:256], T.v2[:], ALU.min, ["v2"], ["pw"], (7,))
+
+    fin = split(T.xf[:], "xf")
+    ts(T.ti[:], T.pw[:], 2048.0, None, ALU.add, None, ["pw"], ["ti"])
+    fin()
+    act(T.hb[:], T.xf[:], ACT.Identity, ["xf"], ["hb"], bias=49152 - 127.5)
+    ts(T.bb[:], T.xf[:], 0.0, 4352.0, ALU.is_lt, ALU.mult, ["xf"], ["bb"])
+    ts(T.ta[:], T.ti[:], 12, 1023, ALU.arith_shift_right, ALU.bitwise_and, ["ti"], ["ta"])
+    cp(T.oc[:], T.ta[:], ["ta"], ["oc"])
+    mm(0, ps[0][:, 0:256], T.idf[:], T.xf[:], True, False, ["idf", "xf"])
+    mm(0, ps[0][:, 0:256], mat("I"), T.bb[:], False, False, ["I", "bb"])
+    mm(0, ps[0][:, 0:256], mat("I"), T.hb[:], False, True, ["I", "hb"])
+    act(T.oe[:], ps[0][:, 0:256], ACT.Identity, [], ["oe"], (0,), bias=-49152.0)
+    deps("s", ["oe"], (), ())
+    g.scalar.dma_start(T.ye[:], T.oe[:]).then_inc(T.sem.sto, 16)
+    deps("y", ["oc"], (), ())
+    g.sync.dma_start(T.yc[:], T.oc[0:128:16, :]).then_inc(T.sem.sto, 16)
+    nsto += 32
+    for q in "vspg":
+        g.wait_ge(T.sem["s" + q], count[q])
+    g.wait_ge(T.sem.sent, sent[0])
+    g.wait_ge(T.sem.sto, nsto)

@@ -23,7 +23,7 @@ SCRATCH = {
     "cvote": _sb(256, "bfloat16"), "csum": _sb(256, "bfloat16"),
     "pw": _sb(256, "float32"), "rr": _sb(256, "float32"), "sc": _sb(256, "float32"), "sc0": _sb(256, "float32"),
     "l1": _sb(16, "int32"), "l2": _sb(16, "int32"), "ql": _sb(16, "uint16"), "l0": _sb(16, "uint16"),
-    "xh": _sb(256, "float16"), "xf": _sb(256, "float32"), "uu": _sb(256, "bfloat16"), "pen": _sb(2048, "bfloat16"),
+    "xh": _sb(256, "float16"), "xf": _sb(256, "float32"), "uu": _sb(256, "float32"), "pen": _sb(2048, "bfloat16"),
     "acc": _sb(256, "float32"), "yy": _sb(256, "float32"), "ti": _sb(256, "int32"), "tj": _sb(256, "int32"), "ta": _sb(256, "int32"),
     "zh": _sb(256, "float16"), "ll": _sb(256, "uint16"), "aw": _sb(256, "float32"), "kg": _sb(256, "float32"),
     "ga": _sb(2048, "bfloat16"), "mx": _sb(2048, "bfloat16"), "xr": _sb(256, "bfloat16"), "w4": _sb(256, "bfloat16"),
@@ -64,7 +64,7 @@ def _routes(cores, topo):
         far = [d for d in cores if not topo.may_write(s, d)]
         near[s] = [c for c in topo.cores_of(s) if c not in cores and topo.die(c) == topo.die(s) and all(topo.may_write(c, d) for d in far)]
         used.update(near[s])
-    first, hand = ({}, {}), {}
+    plan = ({}, {})
     for r, s in enumerate(cores):
         sib = [d for d in cores if d != s and place(d) == place(s)]
         plane = [d for d in cores if topo.same_plane(s, d)]
@@ -76,47 +76,55 @@ def _routes(cores, topo):
         inner = [c for c in topo.cores_of(plane[0]) if c not in cores and c not in used and topo.die(c) == topo.die(s)]
         off = topo.engines(s, mate[0])
         on = [e for e in topo.engines(s, sib[0]) if e not in off]
-        for kind in (0, 1):
-            a, b, c = near[s][kind], mate[kind], inner[0]
-            first[kind][r] = [(b, off[:len(off) // 2]), (c, off[len(off) // 2:]), (a, on[:len(on) // 2]), (sib[0], on[len(on) // 2:])]
-            for relay, dests in ((a, here), (b, there), (c, plane)):
-                en = topo.engines(relay, dests[0])
-                k = len(en) // len(dests)
-                hand.setdefault(relay, []).append((kind, r, [(d, en[i * k:(i + 1) * k]) for i, d in enumerate(dests)]))
-    return first, hand
+        def split(relay, dests):
+            en = topo.engines(relay, dests[0])
+            k = len(en) // len(dests)
+            return [(r, [d], en[i * k:(i + 1) * k]) for i, d in enumerate(dests)]
+
+        a, b, c = near[s][0], mate[0], inner[0]
+        plan[0][s] = [[(r, [b], off[:len(off) // 2]), (r, [c], off[len(off) // 2:]), (r, [a], on[:len(on) // 2]), (r, sib, on[len(on) // 2:])]]
+        for relay, dests in ((a, here), (b, there), (c, plane)):
+            plan[0].setdefault(relay, []).append(split(relay, dests))
+        gate = lambda pair: [near[d][1] for d in pair if topo.die(d) == topo.die(s)][0]
+        mate2 = [c for c in range(WORLD) if topo.mates(c, here[0]) and topo.die(c) == topo.die(s)
+                 and topo.may_write(s, c) and all(topo.may_write(c, d) for d in here)]
+        plan[1][s] = [[(r, [mate[1], mate2[1], gate(plane)], off), (r, sib, on)]]
+        for relay, pair in ((mate[1], there), (mate2[1], here)):
+            call = plan[1].setdefault(relay, [[]])[0]
+            en = topo.engines(relay, gate(pair))
+            k = len(en) // 2
+            call.append((r, [gate(pair)], en[len(call) * k:(len(call) + 1) * k]))
+        for pair in (plane, there, here):
+            plan[1].setdefault(gate(pair), []).append(split(gate(pair), pair))
+    return plan
 
 
-def _send(g, T, topo, core, msg, r, dests):
-    ap = _piece(T, msg, r)
+def _send(g, T, topo, core, msg, call):
     tr = []
-    for d, en in dests:
-        rid, pid = topo.addr(d, core)
-        tr.append(RemoteDMATransfer(dst_ids=[DstId(rid=rid, pnc=pid)], dma_engine_mask=_bits(en), remote_sem=T.sem[msg], src=ap, dst=ap))
+    for r, dests, en in call:
+        ap = _piece(T, msg, r)
+        ids = [DstId(rid=a[0], pnc=a[1]) for a in (topo.addr(d, core) for d in dests)]
+        tr.append(RemoteDMATransfer(dst_ids=ids, dma_engine_mask=_bits(en), remote_sem=T.sem[msg], srcs=[ap], dsts=[ap] * len(dests)))
     g.remote_dma_fused(tr, local_sem=T.sem.sent)
-    return sum(len(en) for d, en in dests)
+    return sum(len(en) for r, dests, en in call)
 
 
 def rank_program(g, core, T, topo):
     cores = list(T.cores)
-    first, hand = _routes(cores, topo)
+    plan = _routes(cores, topo)
     rank = T.rank_of(core)
+    arrive = [sum(len(en) for c in plan[kind] for call in plan[kind][c] for r, dests, en in call if core in dests) for kind in (0, 1)]
     if rank is None:
         sent = 0
         for msg in MSGS:
-            for kind, r, dests in hand.get(core, []):
-                if kind == _kind(msg):
-                    g.wait_ge(T.sem[msg], sum(len(en) for d, en in first[kind][r] if d == core))
-                    sent += _send(g, T, topo, core, msg, r, dests)
+            calls = plan[_kind(msg)].get(core, [])
+            if calls:
+                g.wait_ge(T.sem[msg], arrive[_kind(msg)])
+            for call in calls:
+                sent += _send(g, T, topo, core, msg, call)
         if sent:
             g.wait_ge(T.sem.sent, sent)
         return
-
-    arrive = [0, 0]
-    for kind in (0, 1):
-        arrive[kind] += sum(len(en) for r in first[kind] for d, en in first[kind][r] if d == core)
-    for relay in hand:
-        for kind, r, dests in hand[relay]:
-            arrive[kind] += sum(len(en) for d, en in dests if d == core)
 
     Q = {"v": g.vector, "s": g.scalar, "p": g.tensor, "g": g, "y": g.sync}
     known = {q: {} for q in Q}
@@ -190,7 +198,7 @@ def rank_program(g, core, T, topo):
 
     def send(msg, r):
         deps("g", r, (), ())
-        sent[0] += _send(g, T, topo, core, msg, rank, first[_kind(msg)][rank])
+        sent[0] += _send(g, T, topo, core, msg, plan[_kind(msg)][core][0])
 
     g.sync.dma_start(_piece(T, "xa", rank), T.x0[:, 0:256]).then_inc(T.sem.lxa, 16)
     g.sync.dma_start(_piece(T, "xb", rank), T.x0[:, 256:512]).then_inc(T.sem.lxb, 16)
@@ -250,7 +258,7 @@ def rank_program(g, core, T, topo):
     act(mat("ROW0"), mat("BD"), ACT.Identity, ["BD", "e0s"], ["ROW0"], scale=col("e0s"))
     ts(T.pa1[:], T.km[:], col("jj"), -4 * BIG, ALU.is_equal, ALU.mult, ["km", "jj"], ["pa1"])
     ts(T.pa2[:], T.km[:], col("j1"), BIG, ALU.is_equal, ALU.mult, ["km", "j1"], ["pa2"])
-    ts(mat("NI"), T.jm[:], 0.0, -1.0, ALU.is_equal, ALU.mult, ["jm"], ["NI"])
+    ts(mat("I"), T.jm[:], 0.0, None, ALU.is_equal, None, ["jm"], ["I"])
 
     for k, (a, e) in enumerate(((0, 512), (512, 768))):
         cp(T.nmf[:, a:e], T.nmi[:, a:e], ["nmi%d" % k], ["nmf%d" % k])
@@ -283,7 +291,6 @@ def rank_program(g, core, T, topo):
         ts(mat("DH"), T.jm[:], 0.0, col("hi"), ALU.is_equal, ALU.mult, ["jm", "hi"], ["DH"])
         ts(mat("UP"), T.jm[:], 8.0, col("lo"), ALU.is_equal, ALU.mult, ["jm", "lo"], ["UP"])
         ts(mat("DN"), T.jm[:], -8.0, col("hi"), ALU.is_equal, ALU.mult, ["jm", "hi"], ["DN"])
-        ts(mat("I"), T.jm[:], 0.0, None, ALU.is_equal, None, ["jm"], ["I"])
         ts(col("t0"), col("n15"), -BIG, 2048.0, ALU.mult, ALU.add, ["n15"], ["t0"])
         ts(mat("SH"), T.jm[:], 1.0, col("n15"), ALU.is_equal, ALU.mult, ["jm", "n15"], ["SH"])
         ts(mat("D0"), T.jm[:], 0.0, col("e0"), ALU.is_equal, ALU.mult, ["jm", "e0"], ["D0"])
@@ -299,103 +306,157 @@ def rank_program(g, core, T, topo):
         act(ps[4][:, 0:256], T.rr[:], ACT.Identity, ["rr"], [], (4,), bias=-C35)
         return lambda: tt(xout, T.pw[:], ps[4][:, 0:256], ALU.subtract, ["pw"], [xkey], (4,))
 
+    H2 = (0, 1)
+    hc = lambda buf, h: buf[:, 128 * h:128 * h + 128]
+    h8 = lambda buf, h: buf[:, 8 * h:8 * h + 8]
+    qg = lambda tab, h: tab[:, 0:1024].indirect(h8(T.ql, h))
+    both = lambda key, a, b: res.update({key: (res[a][0] + res[b][0], [])})
+    K = lambda name, h: name + "AB"[h]
+    DELTA = 90 * 2.0 ** -21
+    res["pwA"] = res["pw"]
+    res["pwB"] = (list(res["pw"][0]), [])
     nsto = 0
     for t in range(STEPS):
         last = t == STEPS - 1
-        qg = lambda tab: tab[:, 0:1024].indirect(T.ql[:, 0:16])
-        fin = split(T.xh[:], "xh")
-        op("v", lambda: V.tensor_tensor_scan(T.sc[:], T.pat[:], T.pw[:], 0.0, ALU.add, ALU.max), ["pat", "pw"], ["sc"])
-        ts(T.l1[:], T.sc[:, 15:256:16], 2048.0, None, ALU.add, None, ["sc"], ["l1"])
-        ts(T.l2[:], T.l1[:], 12, 1023, ALU.arith_shift_right, ALU.bitwise_and, ["l1"], ["l2"])
-        cp(T.ql[:], T.l2[:], ["l2"], ["ql"])
-        fin()
-        act(T.uu[:], qg(T.vtab), ACT.Abs, ["vtab", "ql"], ["uu"], bias=-7.5)
+        for h in H2:
+            op("v", lambda: V.tensor_tensor_scan(hc(T.sc, h), hc(T.pat, h), hc(T.pw, h), 0.0, ALU.add, ALU.max), ["pat", K("pw", h)], [K("sc", h)])
+        for h in H2:
+            ts(h8(T.l1, h), T.sc[:, 128 * h + 15:128 * h + 128:16], 2048.0, None, ALU.add, None, [K("sc", h)], [K("l1", h)])
+        for h in H2:
+            ts(hc(T.rr, h), hc(T.pw, h), 0.5, C35, ALU.add, ALU.add, [K("pw", h)], [K("rr", h)])
+            act(ps[4 + h][:, 0:128], hc(T.rr, h), ACT.Identity, [K("rr", h)], [], (4 + h,), bias=-C35)
+            ts(h8(T.l2, h), h8(T.l1, h), 12, 1023, ALU.arith_shift_right, ALU.bitwise_and, [K("l1", h)], [K("l2", h)])
+        for h in H2:
+            cp(h8(T.ql, h), h8(T.l2, h), [K("l2", h)], [K("ql", h)])
+            act(hc(T.uu, h), qg(T.vtab, h), ACT.Abs, ["vtab", K("ql", h)], [K("uu", h)], bias=-7.5 + DELTA)
+        for h in H2:
+            tt(hc(T.xh, h), hc(T.pw, h), ps[4 + h][:, 0:128], ALU.subtract, [K("pw", h)], [K("xh", h)], (4 + h,))
 
         def word():
             if not last:
-                tt(_piece(T, "me%d" % t, rank), qg(T.kyt), T.xh[:], ALU.add, ["kyt", "ql", "xh"], ["own_e%d" % (t + 2)])
+                tt(_piece(T, "me%d" % t, rank), T.kyt[:, 0:1024].indirect(T.ql[:, 0:16]), T.xh[:], ALU.add,
+                   ["kyt", "qlA", "qlB", "xhA", "xhB"], ["own_e%d" % (t + 2)])
 
         if t == 0:
             late_constants()
         else:
             word()
+
+        cb = lambda h, m: (2 * h, 2 * h + 1, 4 + h, 6 + h)[m % 4]
+
+        def names(m):
+            for h in H2:
+                mm(cb(h, m), ps[cb(h, m)][:, 0:128], mat("P%d" % m), hc(T.xh, h), True, False, ["P%d" % m, K("xh", h)])
+
+        for m in range(4):
+            names(m)
         for m in range(8):
-            pm = T.pen[:, 256 * m:256 * (m + 1)]
-            act(pm, T.uu[:], ACT.Abs, ["uu"], ["pen%d" % m], bias=-(m + 0.5) * 2.0 ** 25, scale=2.0 ** 25)
-            bk = m % 4
-            mm(bk, ps[bk][:, 0:256], mat("P%d" % m), T.xh[:], True, False, ["P%d" % m, "xh"])
-            mm(bk, ps[bk][:, 0:256], mat("NI"), pm, False, True, ["NI", "pen%d" % m])
-            if t == 0 and m == 3:
-                code_table(64, (5, 6))
-            if m == 0:
-                cp(T.acc[:], ps[bk][:, 0:256], [], ["acc"], (bk,))
-            else:
-                tt(T.acc[:], ps[bk][:, 0:256], T.acc[:], ALU.max, ["acc"], ["acc"], (bk,))
+            for h in H2:
+                pm = T.pen[:, 256 * m + 128 * h:256 * m + 128 * h + 128]
+                act(pm, hc(T.uu, h), ACT.Square, [K("uu", h)], [K("pen%d" % m, h)], bias=8192 * (DELTA - m - 0.5), scale=8192.0)
+                mm(cb(h, m), ps[cb(h, m)][:, 0:128], mat("I"), pm, False, True, ["I", K("pen%d" % m, h)])
+            for h in H2:
+                if m == 0:
+                    cp(hc(T.acc, h), ps[cb(h, 0)][:, 0:128], [], [K("acc", h)], (cb(h, 0),))
+                else:
+                    tt(hc(T.acc, h), ps[cb(h, m)][:, 0:128], hc(T.acc, h), ALU.min, [K("acc", h)], [K("acc", h)], (cb(h, m),))
+            if 1 <= m <= 4:
+                names(m + 3)
         if t == 0:
-            for h in range(2):
-                act(T.kyt[:, 512 * h:512 * h + 512], ps[5 + h][:], ACT.Identity, [], ["kyt%d" % h], (5 + h,), scale=4096.0)
-            res["kyt"] = (res["kyt0"][0] + res["kyt1"][0], [])
-            code_table(0, (0, 1))
-            for h in range(2):
-                act(T.kidt[:, 512 * h:512 * h + 512], ps[h][:], ACT.Identity, [], ["kidt%d" % h], (h,), scale=4096.0, bias=float(2 ** 22))
-            res["kidt"] = (res["kidt0"][0] + res["kidt1"][0], [])
-        nb = "nb%d" % (t % 2)
-        act(T.kg[:], qg(T.kidt), ACT.Identity, ["kidt", "ql", nb], ["kg"], bias=col(nb))
-        tt(T.yy[:], qg(T.stab), T.acc[:], ALU.mult, ["stab", "ql", "acc"], ["yy"])
-        ts(T.ti[:], T.yy[:], 2.0 ** -13, None, ALU.add, None, ["yy"], ["ti"])
+            code_table(64, (0, 2))
+            for h in H2:
+                act(T.kyt[:, 512 * h:512 * h + 512], ps[2 * h][:], ACT.Identity, [], [K("kyt", h)], (2 * h,), scale=4096.0)
+            both("kyt", "kytA", "kytB")
+        for h in H2:
+            tt(hc(T.ti, h), qg(T.stab, h), hc(T.acc, h), ALU.mult, ["stab", K("ql", h), K("acc", h)], [K("ti", h)])
+        src = "ti"
         if t % 2:
-            ts(T.tj[:], T.ti[:], 2048.0, None, ALU.add, None, ["ti"], ["tj"])
-            ts(T.ta[:], T.tj[:], 4095, None, ALU.bitwise_and, None, ["tj"], ["ta"])
-        else:
-            ts(T.ta[:], T.ti[:], 4095, None, ALU.bitwise_and, None, ["ti"], ["ta"])
-        ts(T.zh[:], T.ta[:], -2048.0, None, ALU.add, None, ["ta"], ["zh"])
-        ev, od = T.zh[:, 0:256:2], T.zh[:, 1:256:2]
-        mm(4, ps[4][:, 0:128], mat("DL"), ev, True, False, ["DL", "zh"])
-        mm(4, ps[4][:, 0:128], mat("UP"), od, False, True, ["UP", "zh"])
-        mm(4, ps[4][:, 128:256], mat("DN"), ev, True, False, ["DN", "zh"])
-        mm(4, ps[4][:, 128:256], mat("DH"), od, False, True, ["DH", "zh"])
-        mm(6, ps[6][:, 0:256], mat("ROW0"), T.zh[:], True, True, ["ROW0", "zh"])
-        ts(T.ll[:], ps[4][:, 0:256], 2048.0, None, ALU.add, None, [], ["ll"], (4,))
-        op("v", lambda: V.tensor_tensor_scan(T.sc0[:], T.pat[:], ps[6][:, 0:256], 0.0, ALU.add, ALU.max), ["pat"], ["sc0"], (6,))
-        ts(T.l0[:], T.sc0[:, 15:256:16], col("t0"), None, ALU.add, None, ["sc0", "t0"], ["l0"])
+            src = "tj"
+            for h in H2:
+                ts(hc(T.tj, h), hc(T.ti, h), 2048.0, None, ALU.add, None, [K("ti", h)], [K("tj", h)])
+        for h in H2:
+            ts(hc(T.ta, h), hc(T[src], h), 4095, None, ALU.bitwise_and, None, [K(src, h)], [K("ta", h)])
+        for h in H2:
+            ts(hc(T.zh, h), hc(T.ta, h), -2048.0, None, ALU.add, None, [K("ta", h)], [K("zh", h)])
+            ev, od = T.zh[:, 128 * h:128 * h + 128:2], T.zh[:, 128 * h + 1:128 * h + 128:2]
+            bk = 4 + h
+            mm(bk, ps[bk][:, 0:64], mat("DL"), ev, True, False, ["DL", K("zh", h)])
+            mm(bk, ps[bk][:, 0:64], mat("UP"), od, False, True, ["UP", K("zh", h)])
+            mm(bk, ps[bk][:, 64:128], mat("DN"), ev, True, False, ["DN", K("zh", h)])
+            mm(bk, ps[bk][:, 64:128], mat("DH"), od, False, True, ["DH", K("zh", h)])
+        for h in H2:
+            mm(2 * h + 1, ps[2 * h + 1][:, 0:128], mat("ROW0"), hc(T.zh, h), True, True, ["ROW0", K("zh", h)])
+        if t == 0:
+            code_table(0, (6, 7))
+            for h in H2:
+                act(T.kidt[:, 512 * h:512 * h + 512], ps[6 + h][:], ACT.Identity, [], [K("kidt", h)], (6 + h,), scale=4096.0, bias=float(2 ** 22))
+            both("kidt", "kidtA", "kidtB")
+        nb = "nb%d" % (t % 2)
+        act(T.kg[:], T.kidt[:, 0:1024].indirect(T.ql[:, 0:16]), ACT.Identity, ["kidt", "qlA", "qlB", nb], ["kg"], bias=col(nb))
+        for h in H2:
+            ts(hc(T.ll, h), ps[4 + h][:, 0:128], 2048.0, None, ALU.add, None, [], [K("ll", h)], (4 + h,))
+        for h in H2:
+            op("v", lambda: V.tensor_tensor_scan(hc(T.sc0, h), hc(T.pat, h), ps[2 * h + 1][:, 0:128], 0.0, ALU.add, ALU.max),
+               ["pat"], [K("sc0", h)], (2 * h + 1,))
+        ts(T.l0[:], T.sc0[:, 15:256:16], col("t0"), None, ALU.add, None, ["sc0A", "sc0B", "t0"], ["l0"])
+        for h in H2:
+            mm(2 * h, ps[2 * h][:, 0:128], mat("ON"), hc(T.csum, h), True, False, ["ON", "csum"])
         if t == 0:
             word()
-        mm(7, ps[7][:, 0:256], mat("SH"), T.xh[:], True, False, ["SH", "xh"])
-        mm(7, ps[7][:, 0:256], mat("D0"), T.nt[:], False, False, ["D0", "nt"])
-        mm(7, ps[7][:, 0:256], T.idf[:], T.kg[:], False, True, ["idf", "kg"])
-        mm(5, ps[5][:, 0:256], mat("ON"), T.csum[:], True, False, ["ON", "csum"])
-        mm(6, ps[6][:, 0:256], mat("ON"), T.cvote[:], True, False, ["ON", "cvote"])
+        for h in H2:
+            mm(6 + h, ps[6 + h][:, 0:128], mat("SH"), hc(T.xh, h), True, False, ["SH", K("xh", h)])
+            mm(6 + h, ps[6 + h][:, 0:128], mat("D0"), hc(T.nt, h), False, False, ["D0", "nt"])
+            mm(6 + h, ps[6 + h][:, 0:128], T.idf[:], hc(T.kg, h), False, True, ["idf", "kg"])
+            mm(2 * h + 1, ps[2 * h + 1][:, 0:128], mat("ON"), hc(T.cvote, h), True, False, ["ON", "cvote"])
 
         have = [xin[t], xin[t + 1], "own_x%d" % t, "own_x%d" % (t + 1)]
         if not last:
             send("me%d" % t, have + ["own_e%d" % (t + 2)])
         win = T.xw[:, BLK * t:BLK * (t + 2)]
         for c in range(8):
-            a = 256 * c
-            act(T.ga[:, a:a + 256], win.indirect(T.ll[:, 128 + 16 * c:144 + 16 * c]), ACT.Copy, have + ["ll"], ["ga%d" % c])
-            tt(T.mx[:, a:a + 256], win.indirect(T.ll[:, 16 * c:16 * c + 16]), T.ga[:, a:a + 256], ALU.max,
-               have + ["ll", "ga%d" % c], ["mx%d" % c])
+            a, h, o = 256 * c, c // 4, 128 * (c // 4) + 16 * (c % 4)
+            act(T.ga[:, a:a + 256], win.indirect(T.ll[:, o + 64:o + 80]), ACT.Copy, have + [K("ll", h)], ["ga%d" % c])
+            tt(T.mx[:, a:a + 256], win.indirect(T.ll[:, o:o + 16]), T.ga[:, a:a + 256], ALU.max,
+               have + [K("ll", h), "ga%d" % c], ["mx%d" % c])
             if c % 2:
                 q = c // 2
                 for k in range(8):
-                    mm(5, ps[5][:, 64 * q:64 * q + 64], mat("I"), T.mx[:, 512 * q + k:512 * q + 512:8], False, q == 3 and k == 7,
-                       ["I", "mx%d" % (c - 1), "mx%d" % c])
-        act(T.xr[:], ps[5][:, 0:256], ACT.Identity, [], ["xr"], (5,), bias=-127.5)
+                    mm(2 * h, ps[2 * h][:, 64 * (q % 2):64 * (q % 2) + 64], mat("I"), T.mx[:, 512 * q + k:512 * q + 512:8], False,
+                       q % 2 == 1 and k == 7, ["I", "mx%d" % (c - 1), "mx%d" % c])
         wap = T.w4[:] if last else _piece(T, "mw%d" % t, rank)
+        wbuf, w0 = (T.w4, 0) if last else (T.xw, BLK * (t + 2) + LANES * rank)
+        wh = lambda h: wbuf[:, w0 + 128 * h:w0 + 128 * h + 128]
         wk = "own_x%d" % (t + 2)
-        tt(wap, ps[5][:, 0:256], T.xr[:], ALU.subtract, ["xr"], [wk], (5,))
+
+        def closure(h):
+            act(hc(T.aw, h), T.ew[:, BLK * t:BLK * (t + 2)].indirect(h8(T.l0, h)), ACT.Copy,
+                [ein[t], ein[t + 1], "own_e%d" % t, "own_e%d" % (t + 1), "l0"], [K("aw", h)])
+
+        act(hc(T.xr, 0), ps[0][:, 0:128], ACT.Identity, [], ["xrA"], (0,), bias=-127.5)
+        act(hc(T.xr, 1), ps[2][:, 0:128], ACT.Identity, [], ["xrB"], (2,), bias=-127.5)
+        closure(0)
+        closure(1)
+        tt(wh(0), ps[0][:, 0:128], hc(T.xr, 0), ALU.subtract, ["xrA"], [K(wk, 0)], (0,))
+        tt(hc(T.yes, 0), qg(T.ztab, 0), wh(0), ALU.is_le, ["ztab", "qlA", K(wk, 0)], ["yesA"])
+        tt(wh(1), ps[2][:, 0:128], hc(T.xr, 1), ALU.subtract, ["xrB"], [K(wk, 1)], (2,))
+        both(wk, K(wk, 0), K(wk, 1))
         if not last:
             send("mw%d" % t, [wk])
         deps("y", [wk], (), ())
         g.sync.dma_start(T.yx[:, 256 * t:256 * (t + 1)], wap).then_inc(T.sem.sto, 16)
         nsto += 16
-        act(T.aw[:], T.ew[:, BLK * t:BLK * (t + 2)].indirect(T.l0[:, 0:16]), ACT.Copy,
-            [ein[t], ein[t + 1], "own_e%d" % t, "own_e%d" % (t + 1), "l0"], ["aw"])
-        tt(T.yes[:], qg(T.ztab), wap, ALU.is_le, ["ztab", "ql", wk], ["yes"])
-        mm(6, ps[6][:, 0:256], mat("ON"), T.yes[:], False, True, ["ON", "yes"])
-        tt(T.v2[:], ps[6][:, 0:256], T.aw[:], ALU.max, ["aw"], ["v2"], (6,))
-        tt(T.pw[:], ps[7][:, 0:256], T.v2[:], ALU.min, ["v2"], ["pw"], (7,))
+        tt(hc(T.yes, 1), qg(T.ztab, 1), wh(1), ALU.is_le, ["ztab", "qlB", K(wk, 1)], ["yesB"])
+        for h in H2:
+            mm(2 * h + 1, ps[2 * h + 1][:, 0:128], mat("ON"), hc(T.yes, h), False, True, ["ON", K("yes", h)])
+        for h in H2:
+            tt(hc(T.v2, h), ps[2 * h + 1][:, 0:128], hc(T.aw, h), ALU.max, [K("aw", h)], [K("v2", h)], (2 * h + 1,))
+        for h in H2:
+            tt(hc(T.pw, h), ps[6 + h][:, 0:128], hc(T.v2, h), ALU.min, [K("v2", h)], [K("pw", h)], (6 + h,))
 
+    both("pw", "pwA", "pwB")
+    both("ti", "tiA", "tiB")
+    both("ta", "taA", "taB")
+    both("rr", "rrA", "rrB")
     fin = split(T.xf[:], "xf")
     ts(T.ti[:], T.pw[:], 2048.0, None, ALU.add, None, ["pw"], ["ti"])
     fin()

@@ -2,7 +2,7 @@ from concourse.bass import DstId, RemoteDMATransfer
 from concourse.mybir import AluOpType as ALU, ActivationFunctionType as ACT
 
 STEPS, LANES, BLK, WORLD = 5, 256, 2048, 256
-MATS = ["I", "NI", "SH", "DL", "DH", "UP", "DN", "D0", "M9", "M85", "ROW0", "BD", "ON", "E8"] + ["P%d" % m for m in range(8)]
+MATS = ["SH", "DL", "DH", "UP", "DN", "M7", "M75", "ON", "E8", "CW", "DD", "AA"] + ["P%d" % m for m in range(8)]
 
 
 def _sb(n, d):
@@ -13,19 +13,20 @@ SCRATCH = {
     "xw": _sb(6 * BLK, "bfloat16"), "ew": _sb(6 * BLK, "float32"),
     "nmi": _sb(768, "int32"), "nmf": _sb(768, "float32"), "nmh": _sb(768, "bfloat16"), "nmr": _sb(768, "bfloat16"),
     "c8i": _sb(768, "int32"), "c8h": _sb(768, "float16"),
-    "cdi": _sb(1024, "int32"), "vtab": _sb(1024, "bfloat16"), "stab": _sb(1024, "bfloat16"), "ztab": _sb(1024, "bfloat16"),
-    "kki": _sb(128, "int32"), "kka": _sb(128, "float16"), "kkb": _sb(128, "float16"),
-    "kidt": _sb(1024, "float32"), "kyt": _sb(1024, "float32"),
-    "pci": _sb(4, "int32"), "cols": _sb(32, "float32"), "jm": _sb(128, "bfloat16"), "gm": _sb(128, "bfloat16"),
-    "ge": _sb(128, "bfloat16"), "km": _sb(256, "bfloat16"), "nt": _sb(256, "bfloat16"),
-    "mats": _sb(128 * len(MATS), "bfloat16"), "idf": _sb(128, "float32"),
-    "pa1": _sb(256, "bfloat16"), "pa2": _sb(256, "bfloat16"), "pat": _sb(256, "float32"),
-    "cvote": _sb(256, "bfloat16"), "csum": _sb(256, "bfloat16"),
-    "pw": _sb(256, "float32"), "rr": _sb(256, "float32"), "sc": _sb(256, "float32"), "sc0": _sb(256, "float32"),
+    "cdi": _sb(1024, "int32"), "vtab": _sb(2048, "bfloat16"), "stab": _sb(2048, "bfloat16"), "ztab": _sb(2048, "bfloat16"),
+    "ktab": _sb(2048, "float32"), "kki": _sb(128, "int32"), "kkh": _sb(128, "float16"),
+    "pci": _sb(4, "int32"), "cols": _sb(8, "float32"), "ones": _sb(160, "bfloat16"), "zw": _sb(160, "bfloat16"),
+    "zrow": _sb(144, "bfloat16"), "z8": _sb(144, "bfloat16"), "km": _sb(128, "bfloat16"), "nt": _sb(256, "bfloat16"),
+    "mats": _sb(128 * len(MATS), "bfloat16"), "idf": _sb(128, "float32"), "qc": _sb(128, "float32"), "qk": _sb(128, "float32"),
+    "qy": _sb(128, "float32"), "pa1": _sb(128, "bfloat16"), "pa2": _sb(128, "bfloat16"), "pat": _sb(128, "bfloat16"),
+    "cpat": _sb(512, "bfloat16"), "cs": _sb(512, "bfloat16"),
+    "cvote": _sb(128, "bfloat16"), "csum": _sb(128, "bfloat16"), "nb0": _sb(128, "bfloat16"), "nb1": _sb(128, "bfloat16"),
+    "pw": _sb(256, "float32"), "rr": _sb(256, "float32"), "sc": _sb(256, "float32"),
+    "sg": _sb(256, "bfloat16"), "zg": _sb(256, "bfloat16"), "kg": _sb(256, "float32"),
     "l1": _sb(16, "int32"), "l2": _sb(16, "int32"), "ql": _sb(16, "uint16"), "l0": _sb(16, "uint16"),
-    "xh": _sb(256, "float16"), "xf": _sb(256, "float32"), "uu": _sb(256, "float32"), "pen": _sb(2048, "bfloat16"),
-    "acc": _sb(256, "float32"), "yy": _sb(256, "float32"), "ti": _sb(256, "int32"), "tj": _sb(256, "int32"), "ta": _sb(256, "int32"),
-    "zh": _sb(256, "float16"), "ll": _sb(256, "uint16"), "aw": _sb(256, "float32"), "kg": _sb(256, "float32"),
+    "xh": _sb(256, "float16"), "xf": _sb(256, "float32"), "uu": _sb(256, "bfloat16"),
+    "acc": _sb(2048, "float32"), "ti": _sb(256, "int32"), "tj": _sb(256, "int32"), "ta": _sb(256, "int32"),
+    "zh": _sb(256, "float16"), "ll": _sb(256, "uint16"), "aw": _sb(256, "float32"),
     "ga": _sb(2048, "bfloat16"), "mx": _sb(2048, "bfloat16"), "xr": _sb(256, "bfloat16"), "w4": _sb(256, "bfloat16"),
     "yes": _sb(256, "bfloat16"), "v2": _sb(256, "float32"),
     "hb": _sb(256, "bfloat16"), "bb": _sb(256, "bfloat16"), "oe": _sb(256, "float32"), "oc": _sb(256, "float32"),
@@ -34,20 +35,21 @@ for _b in range(8):
     SCRATCH["ps%d" % _b] = ("psum", [128, 512], "float32")
 
 MSGS = ["xa", "xb", "ea", "eb"] + [k + str(t) for t in range(STEPS - 1) for k in ("me", "mw")]
-SEMAPHORES = ["sv", "ss", "sp", "sg", "sent", "sto", "lxa", "lxb", "lce", "le", "lc8", "lcd", "lzt", "lkk"] + MSGS
+SEMAPHORES = ["sv", "ss", "sp", "sg", "sent", "sto", "lxa", "lxb", "lce", "le", "lcc", "lc0", "lcd", "lzt", "lkk", "ltw"] + MSGS
+SEMAPHORES += [m + k for m in MSGS if "e" in m for k in "abc"]
 
 
 def _piece(T, msg, r):
     blk = {"xa": 0, "xb": 1, "ea": 0, "eb": 1}.get(msg)
     if blk is None:
         blk = 2 + int(msg[2:])
-    buf = T.xw if _kind(msg) == 0 else T.ew
+    buf = T.ew if _kind(msg) == 1 else T.xw
     a = blk * BLK + r * LANES
     return buf[:, a:a + LANES]
 
 
 def _kind(msg):
-    return 0 if msg[0] == "x" or msg[1] == "w" else 1
+    return 1 if "e" in msg else 2 if msg == "xb" else 0
 
 
 def _bits(engines):
@@ -64,7 +66,7 @@ def _routes(cores, topo):
         far = [d for d in cores if not topo.may_write(s, d)]
         near[s] = [c for c in topo.cores_of(s) if c not in cores and topo.die(c) == topo.die(s) and all(topo.may_write(c, d) for d in far)]
         used.update(near[s])
-    plan = ({}, {})
+    plan = ({}, {}, {})
     for r, s in enumerate(cores):
         sib = [d for d in cores if d != s and place(d) == place(s)]
         plane = [d for d in cores if topo.same_plane(s, d)]
@@ -81,30 +83,36 @@ def _routes(cores, topo):
             k = len(en) // len(dests)
             return [(r, [d], en[i * k:(i + 1) * k]) for i, d in enumerate(dests)]
 
-        a, b, c = near[s][0], mate[0], inner[0]
-        plan[0][s] = [[(r, [b], off[:len(off) // 2]), (r, [c], off[len(off) // 2:]), (r, [a], on[:len(on) // 2]), (r, sib, on[len(on) // 2:])]]
-        for relay, dests in ((a, here), (b, there), (c, plane)):
-            plan[0].setdefault(relay, []).append(split(relay, dests))
+        for kind, a, b, c in ((0, near[s][0], mate[0], inner[0]), (2, near[s][1], mate[1], inner[0])):
+            plan[kind][s] = [[(r, [b], off[:len(off) // 2]), (r, [c], off[len(off) // 2:]), (r, [a], on[:len(on) // 2]), (r, sib, on[len(on) // 2:])]]
+            for relay, dests in ((a, here), (b, there), (c, plane)):
+                plan[kind].setdefault(relay, []).append(split(relay, dests))
         gate = lambda pair: [near[d][1] for d in pair if topo.die(d) == topo.die(s)][0]
         mate2 = [c for c in range(WORLD) if topo.mates(c, here[0]) and topo.die(c) == topo.die(s)
                  and topo.may_write(s, c) and all(topo.may_write(c, d) for d in here)]
-        plan[1][s] = [[(r, [mate[1], mate2[1], gate(plane)], off), (r, sib, on)]]
-        for relay, pair in ((mate[1], there), (mate2[1], here)):
-            call = plan[1].setdefault(relay, [[]])[0]
-            en = topo.engines(relay, gate(pair))
-            k = len(en) // 2
-            call.append((r, [gate(pair)], en[len(call) * k:(len(call) + 1) * k]))
+        plan[1][s] = [[(r, [mate[1]], off[:len(off) // 2]), (r, [mate2[1]], off[len(off) // 2:]), (r, sib, on)]]
+        plan[1].setdefault(mate2[1], []).insert(0, split(mate2[1], [gate(here)]))
+        plan[1].setdefault(mate[1], []).append(split(mate[1], [gate(there), gate(plane)]))
         for pair in (plane, there, here):
-            plan[1].setdefault(gate(pair), []).append(split(gate(pair), pair))
+            calls = plan[1].setdefault(gate(pair), [])
+            calls.insert(0 if pair is here else len(calls), split(gate(pair), pair))
     return plan
 
 
-def _send(g, T, topo, core, msg, call):
+def _sem(T, plan, msg, r, dests):
+    calls = plan[_kind(msg)][dests[0]]
+    if T.rank_of(dests[0]) is not None or len(calls) == 1:
+        return msg
+    return msg + "abc"[[call[0][0] for call in calls].index(r)]
+
+
+def _send(g, T, topo, plan, core, msg, call):
     tr = []
     for r, dests, en in call:
         ap = _piece(T, msg, r)
         ids = [DstId(rid=a[0], pnc=a[1]) for a in (topo.addr(d, core) for d in dests)]
-        tr.append(RemoteDMATransfer(dst_ids=ids, dma_engine_mask=_bits(en), remote_sem=T.sem[msg], srcs=[ap], dsts=[ap] * len(dests)))
+        tr.append(RemoteDMATransfer(dst_ids=ids, dma_engine_mask=_bits(en), remote_sem=T.sem[_sem(T, plan, msg, r, dests)], srcs=[ap],
+                                    dsts=[ap] * len(dests)))
     g.remote_dma_fused(tr, local_sem=T.sem.sent)
     return sum(len(en) for r, dests, en in call)
 
@@ -113,15 +121,16 @@ def rank_program(g, core, T, topo):
     cores = list(T.cores)
     plan = _routes(cores, topo)
     rank = T.rank_of(core)
-    arrive = [sum(len(en) for c in plan[kind] for call in plan[kind][c] for r, dests, en in call if core in dests) for kind in (0, 1)]
+    arrive = [sum(len(en) for c in plan[kind] for call in plan[kind][c] for r, dests, en in call if core in dests) for kind in (0, 1, 2)]
     if rank is None:
         sent = 0
         for msg in MSGS:
-            calls = plan[_kind(msg)].get(core, [])
-            if calls:
-                g.wait_ge(T.sem[msg], arrive[_kind(msg)])
-            for call in calls:
-                sent += _send(g, T, topo, core, msg, call)
+            here = plan[_kind(msg)]
+            for call in here.get(core, []):
+                mine = [r for r, dests, en in call]
+                g.wait_ge(T.sem[_sem(T, plan, msg, mine[0], [core])],
+                          sum(len(en) for c in here for other in here[c] for r, dests, en in other if core in dests and r in mine))
+                sent += _send(g, T, topo, plan, core, msg, call)
         if sent:
             g.wait_ge(T.sem.sent, sent)
         return
@@ -147,7 +156,7 @@ def rank_program(g, core, T, topo):
     def deps(q, r, w, b):
         ev = []
         for k in r:
-            ev += res.get(k, ([], []))[0]
+            ev += res[k][0]
         for k in w:
             ev += res.get(k, ([], []))[0] + res.get(k, ([], []))[1]
         for k in b:
@@ -160,7 +169,7 @@ def rank_program(g, core, T, topo):
         fn().then_inc(T.sem["s" + q], 1)
         e = ("s" + q, count[q], dict(known[q]))
         for k in r:
-            res.setdefault(k, ([], []))[1].append(e)
+            res[k][1].append(e)
         for k in w:
             res[k] = ([e], [])
         for k in b:
@@ -172,9 +181,9 @@ def rank_program(g, core, T, topo):
     V, S, PE = g.vector, g.scalar, g.tensor
     ps = [T["ps%d" % i] for i in range(8)]
 
-    def mat(name):
+    def mat(name, a=0, e=128):
         i = MATS.index(name)
-        return T.mats[:, 128 * i:128 * (i + 1)]
+        return T.mats[a:e, 128 * i:128 * (i + 1)]
 
     def ts(out, in0, s1, s2, o0, o1, r, w, b=()):
         if o1 is None:
@@ -188,291 +197,327 @@ def rank_program(g, core, T, topo):
     def cp(out, in0, r, w, b=()):
         op("v", lambda: V.tensor_copy(out, in0), r, w, b)
 
+    def fill(out, c, w):
+        op("v", lambda: V.memset(out, c), (), w)
+
+    def scan(out, d0, d1, o0, r, w, b=()):
+        op("v", lambda: V.tensor_tensor_scan(out, d0, d1, 0.0, o0, ALU.max), r, w, b)
+
     def act(out, in0, f, r, w, b=(), bias=0.0, scale=1.0):
         op("s", lambda: S.activation(out, in0, f, bias=bias, scale=scale), r, w, b)
+
+    def sfill(out, c, w):
+        act(out, T.ones[:, 0:128], ACT.Identity, ["ones"], w, scale=c)
 
     def mm(bk, out, lhs, rhs, start, stop, r):
         op("p", lambda: PE.matmul(out, lhs, rhs, start, stop), r, (), (bk,))
 
+    def iota(out, pattern, base, cm, w):
+        op("g", lambda: g.iota(out, pattern, base, cm, allow_small_or_imprecise_dtypes=True), (), w)
+
+    def keep(out, in_, pattern, cmp, base, cm, r, w):
+        op("g", lambda: g.affine_select(out, in_, pattern, cmp, 0.0, base, cm), r, w)
+
+    both = lambda key, *parts: res.update({key: ([e for p in parts for e in res[p][0]], [])})
     sent = [0]
 
     def send(msg, r):
         deps("g", r, (), ())
-        sent[0] += _send(g, T, topo, core, msg, plan[_kind(msg)][core][0])
+        sent[0] += _send(g, T, topo, plan, core, msg, plan[_kind(msg)][core][0])
 
     g.sync.dma_start(_piece(T, "xa", rank), T.x0[:, 0:256]).then_inc(T.sem.lxa, 16)
-    g.sync.dma_start(_piece(T, "xb", rank), T.x0[:, 256:512]).then_inc(T.sem.lxb, 16)
     g.scalar.dma_start(T.nmi[:, 0:512], T.ce0[:]).then_inc(T.sem.lce, 16)
-    g.scalar.dma_start(T.nmi[:, 512:768], T.e0[:]).then_inc(T.sem.le, 16)
-    g.scalar.dma_start(T.c8i[0:8, 0:512], T.cc0[:]).then_inc(T.sem.lc8, 16)
-    g.scalar.dma_start(T.c8i[0:8, 512:768], T.c0[:]).then_inc(T.sem.lc8, 16)
+    g.sync.dma_start(_piece(T, "xb", rank), T.x0[:, 256:512]).then_inc(T.sem.lxb, 16)
+    g.scalar.dma_start(T.c8i[0:8, 0:512], T.cc0[:]).then_inc(T.sem.lcc, 16)
+    g.sync.dma_start(T.nmi[:, 512:768], T.e0[:]).then_inc(T.sem.le, 16)
+    g.sync.dma_start(T.c8i[0:8, 512:768], T.c0[:]).then_inc(T.sem.lc0, 16)
     g.sync.dma_start(T.cdi[:], T.cd[:]).then_inc(T.sem.lcd, 16)
-    g.sync.dma_start(T.kki[:, 0:64], T.kid[:]).then_inc(T.sem.lkk, 16)
-    g.sync.dma_start(T.kki[:, 64:128], T.ky[:]).then_inc(T.sem.lkk, 16)
-    g.sync.dma_start(T.ztab[:], T.zt[:]).then_inc(T.sem.lzt, 16)
-    for key, sem, val in (("own_x0", "lxa", 16), ("own_x1", "lxb", 16), ("nmi0", "lce", 16), ("nmi1", "le", 16), ("c8i", "lc8", 32),
-                          ("cdi", "lcd", 16), ("kki", "lkk", 32), ("ztab", "lzt", 16)):
-        landed(key, sem, val)
+    g.sync.dma_start(T.kki[0:128:2, :], T.kid[:]).then_inc(T.sem.lkk, 16)
+    g.sync.dma_start(T.kki[1:128:2, :], T.ky[:]).then_inc(T.sem.lkk, 16)
+    landed("kki", "lkk", 32)
+    for key, sem in (("own_x0", "lxa"), ("own_x1", "lxb"), ("nmi0", "lce"), ("nmi1", "le"), ("c8i0", "lcc"), ("c8i1", "lc0"), ("cdi", "lcd")):
+        landed(key, sem, 16)
     for msg in MSGS:
         landed("in_" + msg, msg, arrive[_kind(msg)])
     xin = ["in_xa", "in_xb"] + ["in_mw%d" % t for t in range(STEPS - 1)]
     ein = ["in_ea", "in_eb"] + ["in_me%d" % t for t in range(STEPS - 1)]
 
+    BIG, C36, EPS = float(2 ** 25), 1.5 * 2.0 ** 36, 2.0 ** -12
+    CN = ["up", "dn", "jj", "j1", "nb"]
+    col = lambda n: T.cols[:, CN.index(n):CN.index(n) + 1]
+    shift = lambda s: T.zw[:, 16 - s:144 - s]
+    I, D0, J16 = shift(0), T.zrow[:, 16:144], [[0, 8], [1, 16]]
+    jji = T.pci[:, 1:2]
+    fill(T.ones[:], 1.0, ["ones"])
+    fill(mat("ON"), float(2 ** 26), ["ON"])
     op("g", lambda: g.iota(T.pci[:, 0:1], [[0, 1]], 0, 1), (), ("pc",))
-    op("g", lambda: g.iota(T.jm[:], [[1, 128]], 0, -1, allow_small_or_imprecise_dtypes=True), (), ("jm",))
-    op("g", lambda: g.iota(T.gm[:], [[1, 8], [0, 16]], 0, 0, allow_small_or_imprecise_dtypes=True), (), ("gm",))
-    op("g", lambda: g.iota(T.km[:], [[0, 16], [1, 16]], 0, 0, allow_small_or_imprecise_dtypes=True), (), ("km",))
+    iota(mat("DD"), [[-16, 8], [0, 16]], 0, 1, ["DD"])
+    keep(T.zw[:], T.ones[:], [[1, 160]], ALU.is_equal, -16, -1, ["ones"], ["I"])
+    keep(mat("E8", 0, 8), mat("ON", 0, 8), [[-1, 8], [0, 16]], ALU.is_equal, 0, 1, ["ON"], ["E8"])
     send("xa", ["own_x0"])
     send("xb", ["own_x1"])
-    op("g", lambda: g.iota(T.nt[:], [[1, 256]], 0, 0, allow_small_or_imprecise_dtypes=True), (), ("nt",))
-
-    BIG, C35, EPS = float(2 ** 23), 1.5 * 2.0 ** 35, 2.0 ** -12
-    op("v", lambda: V.memset(mat("ON"), float(2 ** 24)), (), ("ON",))
-    op("v", lambda: V.memset(T.cvote[:], -127.0 / 256), (), ("cvote",))
-    op("v", lambda: V.memset(T.csum[:], 384.0 * 2.0 ** -24), (), ("csum",))
-    CN = ["gg", "pp", "jj", "lo", "hi", "his", "n15", "e0", "e0s", "j1", "a1", "a2", "uc", "cc", "t0a", "t0", "nb0", "nb1"]
-    col = lambda n: T.cols[:, CN.index(n):CN.index(n) + 1]
-    ts(T.pci[:, 1:2], T.pci[:, 0:1], 15, None, ALU.bitwise_and, None, ["pc"], ["pj"])
-    ts(T.pci[:, 2:3], T.pci[:, 0:1], 4, None, ALU.arith_shift_right, None, ["pc"], ["pg"])
-    cp(col("pp"), T.pci[:, 0:1], ["pc"], ["pp"])
-    ts(mat("M9"), T.jm[:], 0.0, -9.0, ALU.is_equal, ALU.mult, ["jm"], ["M9"])
-    ts(mat("M85"), T.jm[:], 0.0, 8.5, ALU.is_equal, ALU.mult, ["jm"], ["M85"])
-    ts(T.idf[:], T.jm[:], 0.0, None, ALU.is_equal, None, ["jm"], ["idf"])
-    jji = T.pci[:, 1:2]
-    cp(col("gg"), T.pci[:, 2:3], ["pg"], ["gg"])
-    cp(col("jj"), jji, ["pj"], ["jj"])
-    ts(col("a1"), jji, -1.0, 7.0, ALU.mult, ALU.add, ["pj"], ["a1"])
-    ts(col("a2"), jji, -8.0, None, ALU.add, None, ["pj"], ["a2"])
-    ts(col("cc"), jji, 8.0, EPS, ALU.is_ge, ALU.max, ["pj"], ["cc"])
-    ts(col("e0s"), jji, 0.0, EPS, ALU.is_equal, ALU.mult, ["pj"], ["e0s"])
-    ts(mat("E8"), T.gm[:], col("pp"), 4096.0, ALU.is_equal, ALU.mult, ["gm", "pp"], ["E8"])
-    ts(mat("BD"), T.gm[:], col("gg"), 4096.0, ALU.is_equal, ALU.mult, ["gm", "gg"], ["BD"])
-    tt(col("uc"), col("a1"), col("a2"), ALU.max, ["a1", "a2"], ["uc"])
-    ts(col("lo"), jji, 8.0, None, ALU.is_lt, None, ["pj"], ["lo"])
-    ts(col("hi"), jji, 8.0, None, ALU.is_ge, None, ["pj"], ["hi"])
-    ts(col("his"), jji, 8.0, EPS, ALU.is_ge, ALU.mult, ["pj"], ["his"])
-    ts(col("j1"), jji, 1.0, None, ALU.add, None, ["pj"], ["j1"])
-    ts(T.cols[:, 24:32], T.km[:, 0:8], col("uc"), col("cc"), ALU.is_equal, ALU.mult, ["km", "uc", "cc"], ["co"])
+    keep(T.z8[0:8, :], T.ones[0:8, 0:144], [[1, 144]], ALU.is_equal, -16, -16, ["ones"], ["z8"])
+    iota(T.cpat[0:32, :], [[0, 64], [-16, 4], [-6, 2]], -5, 0, ["cpat0"])
+    fill(T.cpat[32:64, 0:512:2], -1.0, ["cpat1"])
+    fill(T.cpat[32:64, 1:512:2], 1.0, ["cpat2"])
+    ts(jji, T.pci[:, 0:1], 15, None, ALU.bitwise_and, None, ["pc"], ["pj"])
+    fill(mat("CW", 0, 32), 32.0, ["CW0"])
+    ts(col("up"), jji, 8.0, EPS, ALU.is_ge, ALU.max, ["pj"], ["up"])
+    fill(mat("CW", 32, 64), 2.0 ** -7, ["CW1"])
+    ts(col("dn"), col("up"), -1.0, None, ALU.mult, None, ["up"], ["dn"])
+    fill(T.cs[:], 0.0, ["cs"])
+    both("CW", "CW0", "CW1")
+    both("cpat", "cpat0", "cpat1", "cpat2")
+    act(mat("AA"), mat("DD"), ACT.Abs, ["DD"], ["AA"], bias=-7.5)
+    act(T.idf[:], I, ACT.Identity, ["I"], ["idf"])
+    act(mat("M7"), I, ACT.Identity, ["I"], ["M7"], scale=7.0)
+    act(mat("M75"), I, ACT.Identity, ["I"], ["M75"], scale=-7.5)
+    sfill(T.qc[:], 8192.0, ["qc"])
+    sfill(T.csum[:], 384.0 * 2.0 ** -26, ["csum"])
+    sfill(T.cvote[:], 1.0 / 128, ["cvote"])
+    sfill(T.nb0[:], float(256 * rank - 2048), ["nb0"])
+    sfill(T.nb1[:], float(256 * rank), ["nb1"])
     for m in range(8):
-        act(mat("P%d" % m), mat("BD"), ACT.Identity, ["BD", "co"], ["P%d" % m], scale=T.cols[:, 24 + m:25 + m])
-    act(mat("ROW0"), mat("BD"), ACT.Identity, ["BD", "e0s"], ["ROW0"], scale=col("e0s"))
-    ts(T.pa1[:], T.km[:], col("jj"), -4 * BIG, ALU.is_equal, ALU.mult, ["km", "jj"], ["pa1"])
-    ts(T.pa2[:], T.km[:], col("j1"), BIG, ALU.is_equal, ALU.mult, ["km", "j1"], ["pa2"])
-    ts(mat("I"), T.jm[:], 0.0, None, ALU.is_equal, None, ["jm"], ["I"])
+        sign = "up" if m % 2 else "dn"
+        ts(mat("P%d" % m), mat("AA"), m + 0.5, col(sign), ALU.is_equal, ALU.mult, ["AA", sign], ["P%d" % m])
+    fill(T.cs[:, 0:512:8], -float(2 ** 30), ["cs"])
+
+    def floor_of(bk):
+        mm(bk, ps[bk][:], mat("CW", 0, 64), T.cpat[0:64, :], True, False, ["CW", "cpat"])
 
     for k, (a, e) in enumerate(((0, 512), (512, 768))):
         cp(T.nmf[:, a:e], T.nmi[:, a:e], ["nmi%d" % k], ["nmf%d" % k])
-        ts(T.c8h[0:8, a:e], T.c8i[0:8, a:e], -96.0, None, ALU.add, None, ["c8i"], ["c8h%d" % k])
+        ts(T.c8h[0:8, a:e], T.c8i[0:8, a:e], (48.0, 0.0)[k], (2.0 ** -13, 1.0)[k], ALU.add, ALU.mult, ["c8i%d" % k], ["c8h%d" % k])
         act(T.nmh[:, a:e], T.nmf[:, a:e], ACT.Identity, ["nmf%d" % k], ["nmh%d" % k], bias=49152 - 127.5)
         act(T.nmr[:, a:e], T.nmf[:, a:e], ACT.Identity, ["nmf%d" % k], ["nmr%d" % k], bias=98304 - 255.5)
-        o = ps[k][:, 0:e - a]
-        i8 = MATS.index("E8") * 128
-        mm(k, o, T.idf[:], T.nmf[:, a:e], True, False, ["idf", "nmf%d" % k])
-        mm(k, o, T.mats[0:8, i8:i8 + 128], T.c8h[0:8, a:e], False, False, ["E8", "c8h%d" % k])
-        mm(k, o, mat("M9"), T.nmh[:, a:e], False, False, ["M9", "nmh%d" % k])
-        mm(k, o, mat("M85"), T.nmr[:, a:e], False, True, ["M85", "nmr%d" % k])
-    act(_piece(T, "ea", rank), ps[0][:, 0:256], ACT.Copy, [], ["own_e0"], (0,))
-    act(_piece(T, "eb", rank), ps[0][:, 256:512], ACT.Copy, [], ["own_e1"], (0,))
-    act(T.pw[:], ps[1][:, 0:256], ACT.Copy, [], ["pw"], (1,))
+        o = ps[4 + k][:, 0:e - a]
+        mm(4 + k, o, T.idf[:], T.nmf[:, a:e], True, False, ["idf", "nmf%d" % k])
+        if k == 0:
+            mm(4, o, mat("E8", 0, 8), T.c8h[0:8, a:e], False, False, ["E8", "c8h0"])
+        else:
+            for s in range(16):
+                mm(6, ps[6][:, 0:16], T.z8[0:8, 16 - s:144 - s], T.c8h[0:8, 512 + s:768:16], s == 0, s == 15, ["z8", "c8h1"])
+        mm(4 + k, o, mat("M7"), T.nmh[:, a:e], False, False, ["M7", "nmh%d" % k])
+        mm(4 + k, o, mat("M75"), T.nmr[:, a:e], False, True, ["M75", "nmr%d" % k])
+    act(_piece(T, "ea", rank), ps[4][:, 0:256], ACT.Identity, [], ["own_e0"], (4,), bias=-2048.0)
+    act(_piece(T, "eb", rank), ps[4][:, 256:512], ACT.Identity, [], ["own_e1"], (4,), bias=-2048.0)
     send("ea", ["own_e0"])
     send("eb", ["own_e1"])
-    tt(T.pat[:], T.pa1[:], T.pa2[:], ALU.add, ["pa1", "pa2"], ["pat"])
-    cp(T.vtab[:], T.cdi[:], ["cdi"], ["vtab"])
+    cp(T.vtab[:, 0:1024], T.cdi[:], ["cdi"], ["vtab"])
+    for bk in range(4):
+        floor_of(bk)
+    cp(T.ql[:], ps[6][:, 0:16], [], ["qlA", "qlB"], (6,))
+    ts(T.xh[:], ps[5][:, 0:256], 48.0 * 8192 - 2048, None, ALU.add, None, [], ["xhA", "xhB"], (5,))
+    cp(T.kkh[:], T.kki[:], ["kki"], ["kkh"])
+    ts(T.stab[:, 0:1024], T.vtab[:, 0:1024], 8.0, EPS, ALU.is_lt, ALU.max, ["vtab"], ["stab"])
+    deps("y", ["nmh1"], (), ())
+    g.sync.dma_start(T.ztab[:, 0:1024], T.zt[:]).then_inc(T.sem.lzt, 16)
+    landed("ztab", "lzt", 16)
+    iota(T.km[:], J16, 0, 0, ["km"])
+    keep(T.qy[:], T.qc[:], [[-16, 8], [0, 16]], ALU.is_equal, -1, 1, ["qc"], ["qy"])
+    for key, s, base, pattern in (("DL", 0, 7, [[0, 8], [-1, 16]]), ("UP", 8, -8, J16), ("DN", -8, 7, [[0, 8], [-1, 16]]), ("DH", 0, -8, J16)):
+        keep(mat(key), shift(s), pattern, ALU.is_ge, base, 0, ["I"], [key])
+    keep(T.qk[:], T.qc[:], [[-16, 8], [0, 16]], ALU.is_equal, 0, 1, ["qc"], ["qk"])
+    keep(T.zrow[:], T.zw[:, 0:144], [[0, 9], [1, 16]], ALU.is_equal, 0, 0, ["I"], ["zrow"])
+    keep(mat("SH"), shift(1), J16, ALU.is_ge, -1, 0, ["I"], ["SH"])
+    iota(T.nt[:], [[1, 256]], 0, 0, ["nt"])
 
-    def late_constants():
-        ts(T.kka[:], T.kki[:], col("lo"), None, ALU.mult, None, ["kki", "lo"], ["kka"])
-        ts(T.kkb[:], T.kki[:], col("his"), None, ALU.mult, None, ["kki", "his"], ["kkb"])
-        ts(T.stab[:], T.vtab[:], 8.0, EPS, ALU.is_lt, ALU.max, ["vtab"], ["stab"])
-        ts(col("n15"), jji, 15.0, None, ALU.is_lt, None, ["pj"], ["n15"])
-        ts(col("e0"), jji, 0.0, None, ALU.is_equal, None, ["pj"], ["e0"])
-        ts(col("nb0"), jji, 0.0, float(256 * rank), ALU.is_equal, ALU.mult, ["pj"], ["nb0"])
-        ts(col("nb1"), jji, 0.0, float(256 * rank - 2048), ALU.is_equal, ALU.mult, ["pj"], ["nb1"])
-        ts(mat("DL"), T.jm[:], 0.0, col("lo"), ALU.is_equal, ALU.mult, ["jm", "lo"], ["DL"])
-        ts(mat("DH"), T.jm[:], 0.0, col("hi"), ALU.is_equal, ALU.mult, ["jm", "hi"], ["DH"])
-        ts(mat("UP"), T.jm[:], 8.0, col("lo"), ALU.is_equal, ALU.mult, ["jm", "lo"], ["UP"])
-        ts(mat("DN"), T.jm[:], -8.0, col("hi"), ALU.is_equal, ALU.mult, ["jm", "hi"], ["DN"])
-        ts(col("t0"), col("n15"), -BIG, 2048.0, ALU.mult, ALU.add, ["n15"], ["t0"])
-        ts(mat("SH"), T.jm[:], 1.0, col("n15"), ALU.is_equal, ALU.mult, ["jm", "n15"], ["SH"])
-        ts(mat("D0"), T.jm[:], 0.0, col("e0"), ALU.is_equal, ALU.mult, ["jm", "e0"], ["D0"])
+    def code_table():
+        for c in range(8):
+            mm(6 + c // 4, ps[6 + c // 4][:, 128 * (c % 4):128 * (c % 4) + 128], shift(-2 * c), T.kkh[:], True, True, ["I", "kkh"])
+        for h in (0, 1):
+            act(T.ktab[:, 512 * h:512 * h + 512], ps[6 + h][:], ACT.Copy, [], ["ktab%d" % h], (6 + h,))
+        both("ktab", "ktab0", "ktab1")
 
-    def code_table(a, banks):
-        for c in range(16):
-            m, src = (7 - c, "kka") if c < 8 else (c - 8, "kkb")
-            bk = banks[c // 8]
-            mm(bk, ps[bk][:, 64 * (c % 8):64 * (c % 8) + 64], mat("P%d" % m), T[src][:, a:a + 64], True, True, ["P%d" % m, src])
-
-    def split(xout, xkey):
-        ts(T.rr[:], T.pw[:], 0.5, C35, ALU.add, ALU.add, ["pw"], ["rr"])
-        act(ps[4][:, 0:256], T.rr[:], ACT.Identity, ["rr"], [], (4,), bias=-C35)
-        return lambda: tt(xout, T.pw[:], ps[4][:, 0:256], ALU.subtract, ["pw"], [xkey], (4,))
+    def scan_pattern():
+        cp(col("jj"), jji, ["pj"], ["jj"])
+        ts(col("j1"), jji, 1.0, None, ALU.add, None, ["pj"], ["j1"])
+        ts(col("nb"), jji, 15.0, -BIG, ALU.is_lt, ALU.mult, ["pj"], ["nb"])
+        ts(T.pa1[:], T.km[:], col("jj"), -4 * BIG, ALU.is_equal, ALU.mult, ["km", "jj"], ["pa1"])
+        ts(T.pa2[:], T.km[:], col("j1"), BIG, ALU.is_equal, ALU.mult, ["km", "j1"], ["pa2"])
+        tt(T.pat[:], T.pa1[:], T.pa2[:], ALU.add, ["pa1", "pa2"], ["pat"])
 
     H2 = (0, 1)
     hc = lambda buf, h: buf[:, 128 * h:128 * h + 128]
     h8 = lambda buf, h: buf[:, 8 * h:8 * h + 8]
-    qg = lambda tab, h: tab[:, 0:1024].indirect(h8(T.ql, h))
-    both = lambda key, a, b: res.update({key: (res[a][0] + res[b][0], [])})
     K = lambda name, h: name + "AB"[h]
-    DELTA = 90 * 2.0 ** -21
-    res["pwA"] = res["pw"]
-    res["pwB"] = (list(res["pw"][0]), [])
+
+    def run(order):
+        for f, a in order:
+            f(a)
+
+    diag = lambda h: scan(hc(T.sc, h), T.pat[:], hc(T.pw, h), ALU.add, ["pat", K("pw", h)], [K("sc", h)])
+    code = lambda h: ts(h8(T.ql, h), T.sc[:, 128 * h + 15:128 * h + 128:16], col("nb"), 2.0 ** -13, ALU.add, ALU.mult, [K("sc", h), "nb", "twice"],
+                        [K("ql", h)])
+    round1 = lambda h: act(hc(T.rr, h), hc(T.pw, h), ACT.Identity, [K("pw", h)], [K("rr", h)], bias=C36)
+    round2 = lambda h: act(ps[4 + h][:, 384:512], hc(T.rr, h), ACT.Identity, [K("rr", h)], [], (4 + h,), bias=-C36)
+    name = lambda h: tt(hc(T.xh, h), hc(T.pw, h), ps[4 + h][:, 384:512], ALU.subtract, [K("pw", h)], [K("xh", h)], (4 + h,))
+    wide = [1024]
+    pair = lambda h: act(hc(T.uu, h), T.vtab[:, 0:wide[0]].indirect(h8(T.ql, h)), ACT.Abs, ["vtab", K("ql", h)], [K("uu", h)],
+                         scale=BIG * EPS, bias=-7.5 * BIG * EPS)
+    look = lambda out, tab, **kw: act(T[out][:], T[tab][:, 0:wide[0]].indirect(T.ql[:, 0:16]), ACT.Identity, [tab, "qlA", "qlB"], [out], **kw)
+
+    def twice(_):
+        tabs = ("vtab", "stab", "ktab", "ztab")
+        deps("y", tabs + ("llA",), (), ())
+        for tab in tabs:
+            g.sync.dma_start(T[tab][:, 1024:2048], T[tab][:, 0:1024]).then_inc(T.sem.ltw, 16)
+        landed("twice", "ltw", 16 * len(tabs))
+        wide[0] = 2048
+
+    pair(0)
+    pair(1)
     nsto = 0
     for t in range(STEPS):
         last = t == STEPS - 1
-        for h in H2:
-            op("v", lambda: V.tensor_tensor_scan(hc(T.sc, h), hc(T.pat, h), hc(T.pw, h), 0.0, ALU.add, ALU.max), ["pat", K("pw", h)], [K("sc", h)])
-        for h in H2:
-            ts(h8(T.l1, h), T.sc[:, 128 * h + 15:128 * h + 128:16], 2048.0, None, ALU.add, None, [K("sc", h)], [K("l1", h)])
-        for h in H2:
-            ts(hc(T.rr, h), hc(T.pw, h), 0.5, C35, ALU.add, ALU.add, [K("pw", h)], [K("rr", h)])
-            act(ps[4 + h][:, 0:128], hc(T.rr, h), ACT.Identity, [K("rr", h)], [], (4 + h,), bias=-C35)
-            ts(h8(T.l2, h), h8(T.l1, h), 12, 1023, ALU.arith_shift_right, ALU.bitwise_and, [K("l1", h)], [K("l2", h)])
-        for h in H2:
-            cp(h8(T.ql, h), h8(T.l2, h), [K("l2", h)], [K("ql", h)])
-            act(hc(T.uu, h), qg(T.vtab, h), ACT.Abs, ["vtab", K("ql", h)], [K("uu", h)], bias=-7.5 + DELTA)
-        for h in H2:
-            tt(hc(T.xh, h), hc(T.pw, h), ps[4 + h][:, 0:128], ALU.subtract, [K("pw", h)], [K("xh", h)], (4 + h,))
-
-        def word():
-            if not last:
-                tt(_piece(T, "me%d" % t, rank), T.kyt[:, 0:1024].indirect(T.ql[:, 0:16]), T.xh[:], ALU.add,
-                   ["kyt", "qlA", "qlB", "xhA", "xhB"], ["own_e%d" % (t + 2)])
-
         if t == 0:
-            late_constants()
-        else:
-            word()
+            code_table()
+            scan_pattern()
+        look("sg", "stab", scale=8192.0)
+        for bk in range(4):
+            h, a = bk // 2, 64 * bk
+            for m in range(8):
+                mm(bk, ps[bk][:, m:512:8], I, T.uu[:, a:a + 64], False, False, ["I", K("uu", h)])
+            for m in range(8):
+                mm(bk, ps[bk][:, m:512:8], mat("P%d" % m), T.xh[:, a:a + 64], False, m == 7, ["P%d" % m, K("xh", h)])
+            if bk > 1:
+                mm(4 + bk, ps[4 + bk][:, 256:384], I, hc(T.sg, bk - 2), True, True, ["I", "sg"])
+        look("kg", "ktab", bias=1024.0)
+        look("zg", "ztab", scale=-1.0)
+        pick = lambda bk: scan(T.acc[:, 512 * bk:512 * bk + 512], T.cs[:], ps[bk][:], ALU.subtract, ["cs"], ["acc%d" % bk], (bk,))
+        half = lambda h: tt(hc(T.ti, h), ps[6 + h][:, 256:384], T.acc[:, 1024 * h + 7:1024 * h + 1024:8], ALU.mult,
+                            ["acc%d" % (2 * h), "acc%d" % (2 * h + 1)], [K("ti", h)], (6 + h,))
+        turn = lambda h: ts(hc(T.tj, h), hc(T.ti, h), (2048.0, 6144.0)[t % 2], None, ALU.add, None, [K("ti", h)], [K("tj", h)])
+        cut = lambda h: ts(hc(T.ta, h), hc(T.tj, h), 1, 4095, ALU.arith_shift_right, ALU.bitwise_and, [K("tj", h)], [K("ta", h)])
 
-        cb = lambda h, m: (2 * h, 2 * h + 1, 4 + h, 6 + h)[m % 4]
-
-        def names(m):
-            for h in H2:
-                mm(cb(h, m), ps[cb(h, m)][:, 0:128], mat("P%d" % m), hc(T.xh, h), True, False, ["P%d" % m, K("xh", h)])
-
-        for m in range(4):
-            names(m)
-        for m in range(8):
-            for h in H2:
-                pm = T.pen[:, 256 * m + 128 * h:256 * m + 128 * h + 128]
-                act(pm, hc(T.uu, h), ACT.Square, [K("uu", h)], [K("pen%d" % m, h)], bias=8192 * (DELTA - m - 0.5), scale=8192.0)
-                mm(cb(h, m), ps[cb(h, m)][:, 0:128], mat("I"), pm, False, True, ["I", K("pen%d" % m, h)])
-            for h in H2:
-                if m == 0:
-                    cp(hc(T.acc, h), ps[cb(h, 0)][:, 0:128], [], [K("acc", h)], (cb(h, 0),))
-                else:
-                    tt(hc(T.acc, h), ps[cb(h, m)][:, 0:128], hc(T.acc, h), ALU.min, [K("acc", h)], [K("acc", h)], (cb(h, m),))
-            if 1 <= m <= 4:
-                names(m + 3)
-        if t == 0:
-            code_table(64, (0, 2))
-            for h in H2:
-                act(T.kyt[:, 512 * h:512 * h + 512], ps[2 * h][:], ACT.Identity, [], [K("kyt", h)], (2 * h,), scale=4096.0)
-            both("kyt", "kytA", "kytB")
-        for h in H2:
-            tt(hc(T.ti, h), qg(T.stab, h), hc(T.acc, h), ALU.mult, ["stab", K("ql", h), K("acc", h)], [K("ti", h)])
-        src = "ti"
-        if t % 2:
-            src = "tj"
-            for h in H2:
-                ts(hc(T.tj, h), hc(T.ti, h), 2048.0, None, ALU.add, None, [K("ti", h)], [K("tj", h)])
-        for h in H2:
-            ts(hc(T.ta, h), hc(T[src], h), 4095, None, ALU.bitwise_and, None, [K(src, h)], [K("ta", h)])
-        for h in H2:
+        def move(h):
             ts(hc(T.zh, h), hc(T.ta, h), -2048.0, None, ALU.add, None, [K("ta", h)], [K("zh", h)])
             ev, od = T.zh[:, 128 * h:128 * h + 128:2], T.zh[:, 128 * h + 1:128 * h + 128:2]
             bk = 4 + h
-            mm(bk, ps[bk][:, 0:64], mat("DL"), ev, True, False, ["DL", K("zh", h)])
-            mm(bk, ps[bk][:, 0:64], mat("UP"), od, False, True, ["UP", K("zh", h)])
-            mm(bk, ps[bk][:, 64:128], mat("DN"), ev, True, False, ["DN", K("zh", h)])
-            mm(bk, ps[bk][:, 64:128], mat("DH"), od, False, True, ["DH", K("zh", h)])
-        for h in H2:
-            mm(2 * h + 1, ps[2 * h + 1][:, 0:128], mat("ROW0"), hc(T.zh, h), True, True, ["ROW0", K("zh", h)])
-        if t == 0:
-            code_table(0, (6, 7))
-            for h in H2:
-                act(T.kidt[:, 512 * h:512 * h + 512], ps[6 + h][:], ACT.Identity, [], [K("kidt", h)], (6 + h,), scale=4096.0, bias=float(2 ** 22))
-            both("kidt", "kidtA", "kidtB")
+            mm(bk, ps[bk][:, 128:192], mat("DL"), ev, True, False, ["DL", K("zh", h)])
+            mm(bk, ps[bk][:, 128:192], mat("UP"), od, False, True, ["UP", K("zh", h)])
+            mm(bk, ps[bk][:, 192:256], mat("DN"), ev, True, False, ["DN", K("zh", h)])
+            mm(bk, ps[bk][:, 192:256], mat("DH"), od, False, True, ["DH", K("zh", h)])
+
+        def word(h):
+            if not last:
+                mm(6 + h, ps[6 + h][:, 384:512], I, hc(T.xh, h), True, False, ["I", K("xh", h)])
+                mm(6 + h, ps[6 + h][:, 384:512], T.qy[:], hc(T.kg, h), False, True, ["qy", "kg"])
+                a = BLK * (t + 2) + LANES * rank + 128 * h
+                act(T.ew[:, a:a + 128], ps[6 + h][:, 384:512], ACT.Identity, [], [K("word", h)], (6 + h,), bias=-float(2 ** 23))
+
+        lists = lambda h: ts(hc(T.ll, h), ps[4 + h][:, 128:256], 2048.0, None, ALU.add, None, [], [K("ll", h)], (4 + h,))
+        again = lambda bk: None if last else floor_of(bk)
         nb = "nb%d" % (t % 2)
-        act(T.kg[:], T.kidt[:, 0:1024].indirect(T.ql[:, 0:16]), ACT.Identity, ["kidt", "qlA", "qlB", nb], ["kg"], bias=col(nb))
-        for h in H2:
-            ts(hc(T.ll, h), ps[4 + h][:, 0:128], 2048.0, None, ALU.add, None, [], [K("ll", h)], (4 + h,))
-        for h in H2:
-            op("v", lambda: V.tensor_tensor_scan(hc(T.sc0, h), hc(T.pat, h), ps[2 * h + 1][:, 0:128], 0.0, ALU.add, ALU.max),
-               ["pat"], [K("sc0", h)], (2 * h + 1,))
-        ts(T.l0[:], T.sc0[:, 15:256:16], col("t0"), None, ALU.add, None, ["sc0A", "sc0B", "t0"], ["l0"])
-        for h in H2:
-            mm(2 * h, ps[2 * h][:, 0:128], mat("ON"), hc(T.csum, h), True, False, ["ON", "csum"])
-        if t == 0:
-            word()
-        for h in H2:
+
+        def bind(h):
             mm(6 + h, ps[6 + h][:, 0:128], mat("SH"), hc(T.xh, h), True, False, ["SH", K("xh", h)])
-            mm(6 + h, ps[6 + h][:, 0:128], mat("D0"), hc(T.nt, h), False, False, ["D0", "nt"])
-            mm(6 + h, ps[6 + h][:, 0:128], T.idf[:], hc(T.kg, h), False, True, ["idf", "kg"])
-            mm(2 * h + 1, ps[2 * h + 1][:, 0:128], mat("ON"), hc(T.cvote, h), True, False, ["ON", "cvote"])
+            mm(6 + h, ps[6 + h][:, 0:128], D0, hc(T.nt, h), False, False, ["zrow", "nt"])
+            mm(6 + h, ps[6 + h][:, 0:128], D0, T[nb][:], False, False, ["zrow", nb])
+            mm(6 + h, ps[6 + h][:, 0:128], T.qk[:], hc(T.kg, h), False, True, ["qk", "kg"])
+
+        def clear(h):
+            mm(4 + h, ps[4 + h][:, 0:128], mat("ON"), T.csum[:], True, False, ["ON", "csum"])
+            mm(6 + h, ps[6 + h][:, 128:256], I, hc(T.zg, h), True, False, ["I", "zg"])
+
+        def spread(_):
+            for s in range(16):
+                mm(3, ps[3][:, 0:16], T.zrow[:, 16 - s:144 - s], T.zh[:, s:256:16], s == 0, s == 15, ["zrow", "zhA", "zhB"])
+
+        run(((pick, 0), (pick, 1), (half, 0), (word, 0), (again, 0), (again, 1), (bind, 0), (pick, 2), (turn, 0), (pick, 3), (again, 2), (cut, 0),
+             (half, 1), (word, 1), (move, 0), (turn, 1), (lists, 0), (bind, 1), (cut, 1), (move, 1), (clear, 0), (spread, 0)))
+        if not last:
+            both("own_e%d" % (t + 2), "wordA", "wordB")
 
         have = [xin[t], xin[t + 1], "own_x%d" % t, "own_x%d" % (t + 1)]
         if not last:
             send("me%d" % t, have + ["own_e%d" % (t + 2)])
         win = T.xw[:, BLK * t:BLK * (t + 2)]
-        for c in range(8):
-            a, h, o = 256 * c, c // 4, 128 * (c // 4) + 16 * (c % 4)
-            act(T.ga[:, a:a + 256], win.indirect(T.ll[:, o + 64:o + 80]), ACT.Copy, have + [K("ll", h)], ["ga%d" % c])
-            tt(T.mx[:, a:a + 256], win.indirect(T.ll[:, o:o + 16]), T.ga[:, a:a + 256], ALU.max,
-               have + [K("ll", h), "ga%d" % c], ["mx%d" % c])
-            if c % 2:
-                q = c // 2
-                for k in range(8):
-                    mm(2 * h, ps[2 * h][:, 64 * (q % 2):64 * (q % 2) + 64], mat("I"), T.mx[:, 512 * q + k:512 * q + 512:8], False,
-                       q % 2 == 1 and k == 7, ["I", "mx%d" % (c - 1), "mx%d" % c])
         wap = T.w4[:] if last else _piece(T, "mw%d" % t, rank)
         wbuf, w0 = (T.w4, 0) if last else (T.xw, BLK * (t + 2) + LANES * rank)
         wh = lambda h: wbuf[:, w0 + 128 * h:w0 + 128 * h + 128]
         wk = "own_x%d" % (t + 2)
 
-        def closure(h):
-            act(hc(T.aw, h), T.ew[:, BLK * t:BLK * (t + 2)].indirect(h8(T.l0, h)), ACT.Copy,
-                [ein[t], ein[t + 1], "own_e%d" % t, "own_e%d" % (t + 1), "l0"], [K("aw", h)])
+        def upper(c):
+            a, h, o = 256 * c, c // 4, 128 * (c // 4) + 16 * (c % 4)
+            act(T.ga[:, a:a + 256], win.indirect(T.ll[:, o + 64:o + 80]), ACT.Copy, have + [K("ll", h)], ["ga%d" % c])
 
-        act(hc(T.xr, 0), ps[0][:, 0:128], ACT.Identity, [], ["xrA"], (0,), bias=-127.5)
-        act(hc(T.xr, 1), ps[2][:, 0:128], ACT.Identity, [], ["xrB"], (2,), bias=-127.5)
-        closure(0)
-        closure(1)
-        tt(wh(0), ps[0][:, 0:128], hc(T.xr, 0), ALU.subtract, ["xrA"], [K(wk, 0)], (0,))
-        tt(hc(T.yes, 0), qg(T.ztab, 0), wh(0), ALU.is_le, ["ztab", "qlA", K(wk, 0)], ["yesA"])
-        tt(wh(1), ps[2][:, 0:128], hc(T.xr, 1), ALU.subtract, ["xrB"], [K(wk, 1)], (2,))
-        both(wk, K(wk, 0), K(wk, 1))
-        if not last:
-            send("mw%d" % t, [wk])
-        deps("y", [wk], (), ())
-        g.sync.dma_start(T.yx[:, 256 * t:256 * (t + 1)], wap).then_inc(T.sem.sto, 16)
+        def lower(c):
+            a, h, o = 256 * c, c // 4, 128 * (c // 4) + 16 * (c % 4)
+            tt(T.mx[:, a:a + 256], win.indirect(T.ll[:, o:o + 16]), T.ga[:, a:a + 256], ALU.max,
+               have + [K("ll", h), "ga%d" % c], ["mx%d" % c])
+
+        def add(q, bk, o):
+            for k in range(8):
+                mm(bk, ps[bk][:, o:o + 64], I, T.mx[:, 512 * q + k:512 * q + 512:8], False,
+                   bk < 6 and q % 2 == 1 and k == 7, ["I", "mx%d" % (2 * q), "mx%d" % (2 * q + 1)])
+
+        sums = lambda q: add(q, 4 + q // 2, 64 * (q % 2))
+        less = lambda q: add(q, 6 + q // 2, 128 + 64 * (q % 2))
+
+        first = lambda _: ts(T.l0[:], ps[3][:, 0:16], 2048.0, None, ALU.add, None, [], ["l0"], (3,))
+        closure = lambda h: act(hc(T.aw, h), T.ew[:, BLK * t:BLK * (t + 2)].indirect(h8(T.l0, h)), ACT.Copy,
+                                [ein[t], ein[t + 1], "own_e%d" % t, "own_e%d" % (t + 1), "l0"], [K("aw", h)])
+        rest = lambda h: act(hc(T.xr, h), ps[4 + h][:, 0:128], ACT.Identity, [], [K("xr", h)], (4 + h,), scale=-1.0, bias=127.5)
+        value = lambda h: tt(wh(h), ps[4 + h][:, 0:128], hc(T.xr, h), ALU.add, [K("xr", h)], [K(wk, h)], (4 + h,))
+        margin = lambda h: mm(6 + h, ps[6 + h][:, 128:256], I, hc(T.xr, h), False, True, ["I", K("xr", h)])
+        reach = lambda h: act(hc(T.yes, h), ps[6 + h][:, 128:256], ACT.Sign, [], [K("yes", h)], (6 + h,), bias=49152.5)
+
+        def vote(h):
+            mm(6 + h, ps[6 + h][:, 256:384], mat("ON"), T.cvote[:], True, False, ["ON", "cvote"])
+            mm(6 + h, ps[6 + h][:, 256:384], mat("ON"), hc(T.yes, h), False, True, ["ON", K("yes", h)])
+
+        def leave(_):
+            both(wk, K(wk, 0), K(wk, 1))
+            if not last:
+                send("mw%d" % t, [wk])
+            deps("y", [wk], (), ())
+            g.sync.dma_start(T.yx[:, 256 * t:256 * (t + 1)], wap).then_inc(T.sem.sto, 16)
+
+        low = lambda h: tt(hc(T.v2, h), ps[6 + h][:, 256:384], hc(T.aw, h), ALU.max, [K("aw", h)], [K("v2", h)], (6 + h,))
+        high = lambda h: tt(hc(T.pw, h), ps[6 + h][:, 0:128], hc(T.v2, h), ALU.min, [K("v2", h)], [K("pw", h)], (6 + h,))
+        if t == 0:
+            twice(0)
+        run(((upper, 0), (lower, 0), (lists, 1), (clear, 1)))
+        for c in range(1, 8):
+            upper(c)
+        run(((lower, 1), (first, 0), (sums, 0), (less, 0), (again, 3), (lower, 2), (lower, 3), (sums, 1), (less, 1), (lower, 4), (lower, 5),
+             (sums, 2), (rest, 0), (margin, 0), (less, 2), (lower, 6), (lower, 7), (sums, 3), (value, 0)))
+        if last:
+            run(((closure, 0), (reach, 0), (vote, 0), (less, 3), (low, 0), (rest, 1), (margin, 1), (closure, 1), (reach, 1), (vote, 1)))
+        else:
+            run(((reach, 0), (vote, 0), (less, 3), (rest, 1), (margin, 1), (value, 1), (leave, 0), (closure, 0), (low, 0), (reach, 1), (vote, 1), (closure, 1)))
         nsto += 16
-        tt(hc(T.yes, 1), qg(T.ztab, 1), wh(1), ALU.is_le, ["ztab", "qlB", K(wk, 1)], ["yesB"])
-        for h in H2:
-            mm(2 * h + 1, ps[2 * h + 1][:, 0:128], mat("ON"), hc(T.yes, h), False, True, ["ON", K("yes", h)])
-        for h in H2:
-            tt(hc(T.v2, h), ps[2 * h + 1][:, 0:128], hc(T.aw, h), ALU.max, [K("aw", h)], [K("v2", h)], (2 * h + 1,))
-        for h in H2:
-            tt(hc(T.pw, h), ps[6 + h][:, 0:128], hc(T.v2, h), ALU.min, [K("v2", h)], [K("pw", h)], (6 + h,))
+        if not last:
+            run(((high, 0), (round1, 0), (diag, 0), (low, 1), (code, 0), (high, 1), (round2, 0), (pair, 0), (round1, 1), (diag, 1), (name, 0),
+                 (code, 1), (round2, 1), (pair, 1), (name, 1)))
 
-    both("pw", "pwA", "pwB")
-    both("ti", "tiA", "tiB")
-    both("ta", "taA", "taB")
-    both("rr", "rrA", "rrB")
-    fin = split(T.xf[:], "xf")
-    ts(T.ti[:], T.pw[:], 2048.0, None, ALU.add, None, ["pw"], ["ti"])
-    fin()
-    act(T.hb[:], T.xf[:], ACT.Identity, ["xf"], ["hb"], bias=49152 - 127.5)
-    ts(T.bb[:], T.xf[:], 0.0, 4352.0, ALU.is_lt, ALU.mult, ["xf"], ["bb"])
-    ts(T.ta[:], T.ti[:], 12, 1023, ALU.arith_shift_right, ALU.bitwise_and, ["ti"], ["ta"])
-    cp(T.oc[:], T.ta[:], ["ta"], ["oc"])
-    mm(0, ps[0][:, 0:256], T.idf[:], T.xf[:], True, False, ["idf", "xf"])
-    mm(0, ps[0][:, 0:256], mat("I"), T.bb[:], False, False, ["I", "bb"])
-    mm(0, ps[0][:, 0:256], mat("I"), T.hb[:], False, True, ["I", "hb"])
-    act(T.oe[:], ps[0][:, 0:256], ACT.Identity, [], ["oe"], (0,), bias=-49152.0)
-    deps("s", ["oe"], (), ())
-    g.scalar.dma_start(T.ye[:], T.oe[:]).then_inc(T.sem.sto, 16)
-    deps("y", ["oc"], (), ())
-    g.sync.dma_start(T.yc[:], T.oc[0:128:16, :]).then_inc(T.sem.sto, 16)
-    nsto += 32
+    whole = lambda h: ts(hc(T.ti, h), hc(T.pw, h), 2.0 ** -13, None, ALU.mult, None, [K("pw", h)], [K("ti", h)])
+    mask = lambda h: ts(hc(T.ta, h), hc(T.ti, h), 1023, None, ALU.bitwise_and, None, [K("ti", h)], [K("ta", h)])
+    plain = lambda h: tt(hc(T.xf, h), hc(T.pw, h), ps[4 + h][:, 384:512], ALU.subtract, [K("pw", h)], [K("xf", h)], (4 + h,))
+    block = lambda h: ts(hc(T.bb, h), hc(T.xf, h), 0.0, -3840.0, ALU.is_ge, ALU.mult, [K("xf", h)], [K("bb", h)])
+    piece = lambda h: act(hc(T.hb, h), hc(T.xf, h), ACT.Identity, [K("xf", h)], [K("hb", h)], bias=49152 - 127.5)
+
+    def names(h):
+        mm(h, ps[h][:, 0:128], T.idf[:], hc(T.xf, h), True, False, ["idf", K("xf", h)])
+        mm(h, ps[h][:, 0:128], I, hc(T.bb, h), False, False, ["I", K("bb", h)])
+        mm(h, ps[h][:, 0:128], I, hc(T.hb, h), False, True, ["I", K("hb", h)])
+
+    def store(h):
+        ts(hc(T.oe, h), ps[h][:, 0:128], 4096.0 - 49152.0, None, ALU.add, None, [], [K("oe", h)], (h,))
+        q = "ys"[h]
+        deps(q, [K("oe", h)], (), ())
+        Q[q].dma_start(T.ye[:, 128 * h:128 * h + 128], hc(T.oe, h)).then_inc(T.sem.sto, 16)
+
+    def codes(_):
+        cp(T.oc[:], T.ta[:], ["taA", "taB"], ["oc"])
+        deps("y", ["oc"], (), ())
+        g.sync.dma_start(T.yc[:], T.oc[0:128:16, :]).then_inc(T.sem.sto, 16)
+
+    run(((high, 0), (round1, 0), (value, 1), (leave, 0), (low, 1), (round2, 0), (high, 1), (round1, 1), (plain, 0), (round2, 1), (block, 0),
+         (piece, 0), (names, 0), (whole, 0), (plain, 1), (piece, 1), (block, 1), (names, 1), (whole, 1), (mask, 0), (mask, 1), (store, 0),
+         (store, 1), (codes, 0)))
+    nsto += 48
     for q in "vspg":
         g.wait_ge(T.sem["s" + q], count[q])
     g.wait_ge(T.sem.sent, sent[0])

from concourse.bass import DstId, RemoteDMATransfer
from concourse.mybir import AluOpType as ALU, ActivationFunctionType as ACT

STEPS, LANES, BLK, WORLD = 5, 256, 2048, 256
MATS = ["SH", "DL", "DH", "UP", "DN", "M7", "M75", "ON", "E8", "CW", "DD", "AA"] + ["P%d" % m for m in range(8)]


def _sb(n, d):
    return ("sbuf", [128, n], d)


SCRATCH = {
    "xw": _sb(6 * BLK, "bfloat16"), "ew": _sb(6 * BLK, "float32"),
    "nmi": _sb(768, "int32"), "nmf": _sb(768, "float32"), "nmh": _sb(768, "bfloat16"), "nmr": _sb(768, "bfloat16"),
    "c8i": _sb(768, "int32"), "c8h": _sb(768, "float16"),
    "cdi": _sb(1024, "int32"), "vtab": _sb(2048, "bfloat16"), "stab": _sb(2048, "bfloat16"), "ztab": _sb(2048, "bfloat16"),
    "ktab": _sb(2048, "float32"), "kki": _sb(128, "int32"), "kkh": _sb(128, "float16"),
    "pci": _sb(4, "int32"), "cols": _sb(8, "float32"), "ones": _sb(160, "bfloat16"), "zw": _sb(160, "bfloat16"),
    "zrow": _sb(144, "bfloat16"), "z8": _sb(144, "bfloat16"), "km": _sb(128, "bfloat16"), "nt": _sb(256, "bfloat16"),
    "mats": _sb(128 * len(MATS), "bfloat16"), "idf": _sb(128, "float32"), "qc": _sb(128, "float32"), "qk": _sb(128, "float32"),
    "qy": _sb(128, "float32"), "pa1": _sb(128, "bfloat16"), "pa2": _sb(128, "bfloat16"), "pat": _sb(128, "bfloat16"),
    "cpat": _sb(512, "bfloat16"), "cs": _sb(512, "bfloat16"),
    "cvote": _sb(128, "bfloat16"), "csum": _sb(128, "bfloat16"), "nb0": _sb(128, "bfloat16"), "nb1": _sb(128, "bfloat16"),
    "pw": _sb(256, "float32"), "rr": _sb(256, "float32"), "sc": _sb(256, "float32"),
    "sg": _sb(256, "bfloat16"), "zg": _sb(256, "bfloat16"), "kg": _sb(256, "float32"),
    "l1": _sb(16, "int32"), "l2": _sb(16, "int32"), "ql": _sb(16, "uint16"), "l0": _sb(16, "uint16"),
    "xh": _sb(256, "float16"), "xf": _sb(256, "float32"), "uu": _sb(256, "bfloat16"),
    "acc": _sb(2048, "float32"), "ti": _sb(256, "int32"), "tj": _sb(256, "int32"), "ta": _sb(256, "int32"),
    "zh": _sb(256, "float16"), "ll": _sb(256, "uint16"), "aw": _sb(256, "float32"),
    "ga": _sb(2048, "bfloat16"), "mx": _sb(2048, "bfloat16"), "xr": _sb(256, "bfloat16"), "w4": _sb(256, "bfloat16"),
    "yes": _sb(256, "bfloat16"), "v2": _sb(256, "float32"),
    "hb": _sb(256, "bfloat16"), "bb": _sb(256, "bfloat16"), "oe": _sb(256, "float32"), "oc": _sb(256, "float32"),
}
for _b in range(8):
    SCRATCH["ps%d" % _b] = ("psum", [128, 512], "float32")

MSGS = ["xa", "xb", "ea", "eb"] + [k + str(t) for t in range(STEPS - 1) for k in ("me", "mw")]
SEMAPHORES = ["sv", "ss", "sp", "sg", "sent", "sto", "lxa", "lxb", "lce", "le", "lcc", "lc0", "lcd", "lzt", "lkk", "ltw"] + MSGS
SEMAPHORES += [m + k for m in MSGS if "e" in m for k in "abc"]


def _piece(T, msg, r):
    blk = {"xa": 0, "xb": 1, "ea": 0, "eb": 1}.get(msg)
    if blk is None:
        blk = 2 + int(msg[2:])
    buf = T.ew if _kind(msg) == 1 else T.xw
    a = blk * BLK + r * LANES
    return buf[:, a:a + LANES]


def _kind(msg):
    return 1 if "e" in msg else 2 if msg == "xb" else 0


def _bits(engines):
    m = 0
    for e in engines:
        m |= 1 << e
    return m


def _routes(cores, topo):
    place = lambda c: (topo.host(c), topo.chip(c))
    near, used = {}, set()
    for s in cores:
        far = [d for d in cores if not topo.may_write(s, d)]
        near[s] = [c for c in topo.cores_of(s) if c not in cores and topo.die(c) == topo.die(s) and all(topo.may_write(c, d) for d in far)]
        used.update(near[s])
    plan = ({}, {}, {})
    for r, s in enumerate(cores):
        sib = [d for d in cores if d != s and place(d) == place(s)]
        plane = [d for d in cores if topo.same_plane(s, d)]
        far = [d for d in cores if not topo.may_write(s, d)]
        here = [d for d in far if topo.host(d) == topo.host(s)]
        there = [d for d in far if topo.host(d) != topo.host(s)]
        mate = [c for c in range(WORLD) if topo.mates(c, there[0]) and topo.die(c) == topo.die(s)
                and topo.may_write(s, c) and all(topo.may_write(c, d) for d in there)]
        inner = [c for c in topo.cores_of(plane[0]) if c not in cores and c not in used and topo.die(c) == topo.die(s)]
        off = topo.engines(s, mate[0])
        on = [e for e in topo.engines(s, sib[0]) if e not in off]
        def split(relay, dests):
            en = topo.engines(relay, dests[0])
            k = len(en) // len(dests)
            return [(r, [d], en[i * k:(i + 1) * k]) for i, d in enumerate(dests)]

        for kind, a, b, c in ((0, near[s][0], mate[0], inner[0]), (2, near[s][1], mate[1], inner[0])):
            plan[kind][s] = [[(r, [b], off[:len(off) // 2]), (r, [c], off[len(off) // 2:]), (r, [a], on[:len(on) // 2]), (r, sib, on[len(on) // 2:])]]
            for relay, dests in ((a, here), (b, there), (c, plane)):
                plan[kind].setdefault(relay, []).append(split(relay, dests))
        gate = lambda pair: [near[d][1] for d in pair if topo.die(d) == topo.die(s)][0]
        mate2 = [c for c in range(WORLD) if topo.mates(c, here[0]) and topo.die(c) == topo.die(s)
                 and topo.may_write(s, c) and all(topo.may_write(c, d) for d in here)]
        plan[1][s] = [[(r, [mate[1]], off[:len(off) // 2]), (r, [mate2[1]], off[len(off) // 2:]), (r, sib, on)]]
        plan[1].setdefault(mate2[1], []).insert(0, split(mate2[1], [gate(here)]))
        plan[1].setdefault(mate[1], []).append(split(mate[1], [gate(there), gate(plane)]))
        for pair in (plane, there, here):
            calls = plan[1].setdefault(gate(pair), [])
            calls.insert(0 if pair is here else len(calls), split(gate(pair), pair))
    return plan


def _sem(T, plan, msg, r, dests):
    calls = plan[_kind(msg)][dests[0]]
    if T.rank_of(dests[0]) is not None or len(calls) == 1:
        return msg
    return msg + "abc"[[call[0][0] for call in calls].index(r)]


def _send(g, T, topo, plan, core, msg, call):
    tr = []
    for r, dests, en in call:
        ap = _piece(T, msg, r)
        ids = [DstId(rid=a[0], pnc=a[1]) for a in (topo.addr(d, core) for d in dests)]
        tr.append(RemoteDMATransfer(dst_ids=ids, dma_engine_mask=_bits(en), remote_sem=T.sem[_sem(T, plan, msg, r, dests)], srcs=[ap],
                                    dsts=[ap] * len(dests)))
    g.remote_dma_fused(tr, local_sem=T.sem.sent)
    return sum(len(en) for r, dests, en in call)


def rank_program(g, core, T, topo):
    cores = list(T.cores)
    plan = _routes(cores, topo)
    rank = T.rank_of(core)
    arrive = [sum(len(en) for c in plan[kind] for call in plan[kind][c] for r, dests, en in call if core in dests) for kind in (0, 1, 2)]
    if rank is None:
        sent = 0
        for msg in MSGS:
            here = plan[_kind(msg)]
            for call in here.get(core, []):
                mine = [r for r, dests, en in call]
                g.wait_ge(T.sem[_sem(T, plan, msg, mine[0], [core])],
                          sum(len(en) for c in here for other in here[c] for r, dests, en in other if core in dests and r in mine))
                sent += _send(g, T, topo, plan, core, msg, call)
        if sent:
            g.wait_ge(T.sem.sent, sent)
        return

    Q = {"v": g.vector, "s": g.scalar, "p": g.tensor, "g": g, "y": g.sync}
    known = {q: {} for q in Q}
    count = {q: 0 for q in Q}
    res, bank = {}, {}

    def need(q, events):
        want = {}
        for sem, val, clock in events:
            if known[q].get(sem, 0) < val and want.get(sem, (0, None))[0] < val:
                want[sem] = (val, clock)
        for sem in sorted(want, key=lambda s: -len(want[s][1])):
            val, clock = want[sem]
            if known[q].get(sem, 0) < val:
                Q[q].wait_ge(T.sem[sem], val)
                known[q][sem] = val
                for k in clock:
                    known[q][k] = max(known[q].get(k, 0), clock[k])

    def deps(q, r, w, b):
        ev = []
        for k in r:
            ev += res[k][0]
        for k in w:
            ev += res.get(k, ([], []))[0] + res.get(k, ([], []))[1]
        for k in b:
            ev += [e for qq, e in bank.get(k, {}).items() if qq != q]
        need(q, ev)

    def op(q, fn, r=(), w=(), b=()):
        deps(q, r, w, b)
        count[q] += 1
        fn().then_inc(T.sem["s" + q], 1)
        e = ("s" + q, count[q], dict(known[q]))
        for k in r:
            res[k][1].append(e)
        for k in w:
            res[k] = ([e], [])
        for k in b:
            bank.setdefault(k, {})[q] = e

    def landed(key, sem, val):
        res[key] = ([(sem, val, {})], [])

    V, S, PE = g.vector, g.scalar, g.tensor
    ps = [T["ps%d" % i] for i in range(8)]

    def mat(name, a=0, e=128):
        i = MATS.index(name)
        return T.mats[a:e, 128 * i:128 * (i + 1)]

    def ts(out, in0, s1, s2, o0, o1, r, w, b=()):
        if o1 is None:
            op("v", lambda: V.tensor_scalar(out, in0, s1, None, o0), r, w, b)
        else:
            op("v", lambda: V.tensor_scalar(out, in0, s1, s2, o0, o1), r, w, b)

    def tt(out, in0, in1, o, r, w, b=()):
        op("v", lambda: V.tensor_tensor(out, in0, in1, o), r, w, b)

    def cp(out, in0, r, w, b=()):
        op("v", lambda: V.tensor_copy(out, in0), r, w, b)

    def fill(out, c, w):
        op("v", lambda: V.memset(out, c), (), w)

    def scan(out, d0, d1, o0, r, w, b=()):
        op("v", lambda: V.tensor_tensor_scan(out, d0, d1, 0.0, o0, ALU.max), r, w, b)

    def act(out, in0, f, r, w, b=(), bias=0.0, scale=1.0):
        op("s", lambda: S.activation(out, in0, f, bias=bias, scale=scale), r, w, b)

    def sfill(out, c, w):
        act(out, T.ones[:, 0:128], ACT.Identity, ["ones"], w, scale=c)

    def mm(bk, out, lhs, rhs, start, stop, r):
        op("p", lambda: PE.matmul(out, lhs, rhs, start, stop), r, (), (bk,))

    def iota(out, pattern, base, cm, w):
        op("g", lambda: g.iota(out, pattern, base, cm, allow_small_or_imprecise_dtypes=True), (), w)

    def keep(out, in_, pattern, cmp, base, cm, r, w):
        op("g", lambda: g.affine_select(out, in_, pattern, cmp, 0.0, base, cm), r, w)

    both = lambda key, *parts: res.update({key: ([e for p in parts for e in res[p][0]], [])})
    sent = [0]

    def send(msg, r):
        deps("g", r, (), ())
        sent[0] += _send(g, T, topo, plan, core, msg, plan[_kind(msg)][core][0])

    g.sync.dma_start(_piece(T, "xa", rank), T.x0[:, 0:256]).then_inc(T.sem.lxa, 16)
    g.scalar.dma_start(T.nmi[:, 0:512], T.ce0[:]).then_inc(T.sem.lce, 16)
    g.sync.dma_start(_piece(T, "xb", rank), T.x0[:, 256:512]).then_inc(T.sem.lxb, 16)
    g.scalar.dma_start(T.c8i[0:8, 0:512], T.cc0[:]).then_inc(T.sem.lcc, 16)
    g.sync.dma_start(T.nmi[:, 512:768], T.e0[:]).then_inc(T.sem.le, 16)
    g.sync.dma_start(T.c8i[0:8, 512:768], T.c0[:]).then_inc(T.sem.lc0, 16)
    g.sync.dma_start(T.cdi[:], T.cd[:]).then_inc(T.sem.lcd, 16)
    g.sync.dma_start(T.kki[0:128:2, :], T.kid[:]).then_inc(T.sem.lkk, 16)
    g.sync.dma_start(T.kki[1:128:2, :], T.ky[:]).then_inc(T.sem.lkk, 16)
    landed("kki", "lkk", 32)
    for key, sem in (("own_x0", "lxa"), ("own_x1", "lxb"), ("nmi0", "lce"), ("nmi1", "le"), ("c8i0", "lcc"), ("c8i1", "lc0"), ("cdi", "lcd")):
        landed(key, sem, 16)
    for msg in MSGS:
        landed("in_" + msg, msg, arrive[_kind(msg)])
    xin = ["in_xa", "in_xb"] + ["in_mw%d" % t for t in range(STEPS - 1)]
    ein = ["in_ea", "in_eb"] + ["in_me%d" % t for t in range(STEPS - 1)]

    BIG, C36, EPS = float(2 ** 25), 1.5 * 2.0 ** 36, 2.0 ** -12
    CN = ["up", "dn", "jj", "j1", "nb"]
    col = lambda n: T.cols[:, CN.index(n):CN.index(n) + 1]
    shift = lambda s: T.zw[:, 16 - s:144 - s]
    I, D0, J16 = shift(0), T.zrow[:, 16:144], [[0, 8], [1, 16]]
    jji = T.pci[:, 1:2]
    fill(T.ones[:], 1.0, ["ones"])
    fill(mat("ON"), float(2 ** 26), ["ON"])
    op("g", lambda: g.iota(T.pci[:, 0:1], [[0, 1]], 0, 1), (), ("pc",))
    iota(mat("DD"), [[-16, 8], [0, 16]], 0, 1, ["DD"])
    keep(T.zw[:], T.ones[:], [[1, 160]], ALU.is_equal, -16, -1, ["ones"], ["I"])
    keep(mat("E8", 0, 8), mat("ON", 0, 8), [[-1, 8], [0, 16]], ALU.is_equal, 0, 1, ["ON"], ["E8"])
    send("xa", ["own_x0"])
    send("xb", ["own_x1"])
    keep(T.z8[0:8, :], T.ones[0:8, 0:144], [[1, 144]], ALU.is_equal, -16, -16, ["ones"], ["z8"])
    iota(T.cpat[0:32, :], [[0, 64], [-16, 4], [-6, 2]], -5, 0, ["cpat0"])
    fill(T.cpat[32:64, 0:512:2], -1.0, ["cpat1"])
    fill(T.cpat[32:64, 1:512:2], 1.0, ["cpat2"])
    ts(jji, T.pci[:, 0:1], 15, None, ALU.bitwise_and, None, ["pc"], ["pj"])
    fill(mat("CW", 0, 32), 32.0, ["CW0"])
    ts(col("up"), jji, 8.0, EPS, ALU.is_ge, ALU.max, ["pj"], ["up"])
    fill(mat("CW", 32, 64), 2.0 ** -7, ["CW1"])
    ts(col("dn"), col("up"), -1.0, None, ALU.mult, None, ["up"], ["dn"])
    fill(T.cs[:], 0.0, ["cs"])
    both("CW", "CW0", "CW1")
    both("cpat", "cpat0", "cpat1", "cpat2")
    act(mat("AA"), mat("DD"), ACT.Abs, ["DD"], ["AA"], bias=-7.5)
    act(T.idf[:], I, ACT.Identity, ["I"], ["idf"])
    act(mat("M7"), I, ACT.Identity, ["I"], ["M7"], scale=7.0)
    act(mat("M75"), I, ACT.Identity, ["I"], ["M75"], scale=-7.5)
    sfill(T.qc[:], 8192.0, ["qc"])
    sfill(T.csum[:], 384.0 * 2.0 ** -26, ["csum"])
    sfill(T.cvote[:], 1.0 / 128, ["cvote"])
    sfill(T.nb0[:], float(256 * rank - 2048), ["nb0"])
    sfill(T.nb1[:], float(256 * rank), ["nb1"])
    for m in range(8):
        sign = "up" if m % 2 else "dn"
        ts(mat("P%d" % m), mat("AA"), m + 0.5, col(sign), ALU.is_equal, ALU.mult, ["AA", sign], ["P%d" % m])
    fill(T.cs[:, 0:512:8], -float(2 ** 30), ["cs"])

    def floor_of(bk):
        mm(bk, ps[bk][:], mat("CW", 0, 64), T.cpat[0:64, :], True, False, ["CW", "cpat"])

    for k, (a, e) in enumerate(((0, 512), (512, 768))):
        cp(T.nmf[:, a:e], T.nmi[:, a:e], ["nmi%d" % k], ["nmf%d" % k])
        ts(T.c8h[0:8, a:e], T.c8i[0:8, a:e], (48.0, 0.0)[k], (2.0 ** -13, 1.0)[k], ALU.add, ALU.mult, ["c8i%d" % k], ["c8h%d" % k])
        act(T.nmh[:, a:e], T.nmf[:, a:e], ACT.Identity, ["nmf%d" % k], ["nmh%d" % k], bias=49152 - 127.5)
        act(T.nmr[:, a:e], T.nmf[:, a:e], ACT.Identity, ["nmf%d" % k], ["nmr%d" % k], bias=98304 - 255.5)
        o = ps[4 + k][:, 0:e - a]
        mm(4 + k, o, T.idf[:], T.nmf[:, a:e], True, False, ["idf", "nmf%d" % k])
        if k == 0:
            mm(4, o, mat("E8", 0, 8), T.c8h[0:8, a:e], False, False, ["E8", "c8h0"])
        else:
            for s in range(16):
                mm(6, ps[6][:, 0:16], T.z8[0:8, 16 - s:144 - s], T.c8h[0:8, 512 + s:768:16], s == 0, s == 15, ["z8", "c8h1"])
        mm(4 + k, o, mat("M7"), T.nmh[:, a:e], False, False, ["M7", "nmh%d" % k])
        mm(4 + k, o, mat("M75"), T.nmr[:, a:e], False, True, ["M75", "nmr%d" % k])
    act(_piece(T, "ea", rank), ps[4][:, 0:256], ACT.Identity, [], ["own_e0"], (4,), bias=-2048.0)
    act(_piece(T, "eb", rank), ps[4][:, 256:512], ACT.Identity, [], ["own_e1"], (4,), bias=-2048.0)
    send("ea", ["own_e0"])
    send("eb", ["own_e1"])
    cp(T.vtab[:, 0:1024], T.cdi[:], ["cdi"], ["vtab"])
    for bk in range(4):
        floor_of(bk)
    cp(T.ql[:], ps[6][:, 0:16], [], ["qlA", "qlB"], (6,))
    ts(T.xh[:], ps[5][:, 0:256], 48.0 * 8192 - 2048, None, ALU.add, None, [], ["xhA", "xhB"], (5,))
    cp(T.kkh[:], T.kki[:], ["kki"], ["kkh"])
    ts(T.stab[:, 0:1024], T.vtab[:, 0:1024], 8.0, EPS, ALU.is_lt, ALU.max, ["vtab"], ["stab"])
    deps("y", ["nmh1"], (), ())
    g.sync.dma_start(T.ztab[:, 0:1024], T.zt[:]).then_inc(T.sem.lzt, 16)
    landed("ztab", "lzt", 16)
    iota(T.km[:], J16, 0, 0, ["km"])
    keep(T.qy[:], T.qc[:], [[-16, 8], [0, 16]], ALU.is_equal, -1, 1, ["qc"], ["qy"])
    for key, s, base, pattern in (("DL", 0, 7, [[0, 8], [-1, 16]]), ("UP", 8, -8, J16), ("DN", -8, 7, [[0, 8], [-1, 16]]), ("DH", 0, -8, J16)):
        keep(mat(key), shift(s), pattern, ALU.is_ge, base, 0, ["I"], [key])
    keep(T.qk[:], T.qc[:], [[-16, 8], [0, 16]], ALU.is_equal, 0, 1, ["qc"], ["qk"])
    keep(T.zrow[:], T.zw[:, 0:144], [[0, 9], [1, 16]], ALU.is_equal, 0, 0, ["I"], ["zrow"])
    keep(mat("SH"), shift(1), J16, ALU.is_ge, -1, 0, ["I"], ["SH"])
    iota(T.nt[:], [[1, 256]], 0, 0, ["nt"])

    def code_table():
        for c in range(8):
            mm(6 + c // 4, ps[6 + c // 4][:, 128 * (c % 4):128 * (c % 4) + 128], shift(-2 * c), T.kkh[:], True, True, ["I", "kkh"])
        for h in (0, 1):
            act(T.ktab[:, 512 * h:512 * h + 512], ps[6 + h][:], ACT.Copy, [], ["ktab%d" % h], (6 + h,))
        both("ktab", "ktab0", "ktab1")

    def scan_pattern():
        cp(col("jj"), jji, ["pj"], ["jj"])
        ts(col("j1"), jji, 1.0, None, ALU.add, None, ["pj"], ["j1"])
        ts(col("nb"), jji, 15.0, -BIG, ALU.is_lt, ALU.mult, ["pj"], ["nb"])
        ts(T.pa1[:], T.km[:], col("jj"), -4 * BIG, ALU.is_equal, ALU.mult, ["km", "jj"], ["pa1"])
        ts(T.pa2[:], T.km[:], col("j1"), BIG, ALU.is_equal, ALU.mult, ["km", "j1"], ["pa2"])
        tt(T.pat[:], T.pa1[:], T.pa2[:], ALU.add, ["pa1", "pa2"], ["pat"])

    H2 = (0, 1)
    hc = lambda buf, h: buf[:, 128 * h:128 * h + 128]
    h8 = lambda buf, h: buf[:, 8 * h:8 * h + 8]
    K = lambda name, h: name + "AB"[h]

    def run(order):
        for f, a in order:
            f(a)

    diag = lambda h: scan(hc(T.sc, h), T.pat[:], hc(T.pw, h), ALU.add, ["pat", K("pw", h)], [K("sc", h)])
    code = lambda h: ts(h8(T.ql, h), T.sc[:, 128 * h + 15:128 * h + 128:16], col("nb"), 2.0 ** -13, ALU.add, ALU.mult, [K("sc", h), "nb", "twice"],
                        [K("ql", h)])
    round1 = lambda h: act(hc(T.rr, h), hc(T.pw, h), ACT.Identity, [K("pw", h)], [K("rr", h)], bias=C36)
    round2 = lambda h: act(ps[4 + h][:, 384:512], hc(T.rr, h), ACT.Identity, [K("rr", h)], [], (4 + h,), bias=-C36)
    name = lambda h: tt(hc(T.xh, h), hc(T.pw, h), ps[4 + h][:, 384:512], ALU.subtract, [K("pw", h)], [K("xh", h)], (4 + h,))
    wide = [1024]
    pair = lambda h: act(hc(T.uu, h), T.vtab[:, 0:wide[0]].indirect(h8(T.ql, h)), ACT.Abs, ["vtab", K("ql", h)], [K("uu", h)],
                         scale=BIG * EPS, bias=-7.5 * BIG * EPS)
    look = lambda out, tab, **kw: act(T[out][:], T[tab][:, 0:wide[0]].indirect(T.ql[:, 0:16]), ACT.Identity, [tab, "qlA", "qlB"], [out], **kw)

    def twice(_):
        tabs = ("vtab", "stab", "ktab", "ztab")
        deps("y", tabs + ("llA",), (), ())
        for tab in tabs:
            g.sync.dma_start(T[tab][:, 1024:2048], T[tab][:, 0:1024]).then_inc(T.sem.ltw, 16)
        landed("twice", "ltw", 16 * len(tabs))
        wide[0] = 2048

    pair(0)
    pair(1)
    nsto = 0
    for t in range(STEPS):
        last = t == STEPS - 1
        if t == 0:
            code_table()
            scan_pattern()
        look("sg", "stab", scale=8192.0)
        for bk in range(4):
            h, a = bk // 2, 64 * bk
            for m in range(8):
                mm(bk, ps[bk][:, m:512:8], I, T.uu[:, a:a + 64], False, False, ["I", K("uu", h)])
            for m in range(8):
                mm(bk, ps[bk][:, m:512:8], mat("P%d" % m), T.xh[:, a:a + 64], False, m == 7, ["P%d" % m, K("xh", h)])
            if bk > 1:
                mm(4 + bk, ps[4 + bk][:, 256:384], I, hc(T.sg, bk - 2), True, True, ["I", "sg"])
        look("kg", "ktab", bias=1024.0)
        look("zg", "ztab", scale=-1.0)
        pick = lambda bk: scan(T.acc[:, 512 * bk:512 * bk + 512], T.cs[:], ps[bk][:], ALU.subtract, ["cs"], ["acc%d" % bk], (bk,))
        half = lambda h: tt(hc(T.ti, h), ps[6 + h][:, 256:384], T.acc[:, 1024 * h + 7:1024 * h + 1024:8], ALU.mult,
                            ["acc%d" % (2 * h), "acc%d" % (2 * h + 1)], [K("ti", h)], (6 + h,))
        turn = lambda h: ts(hc(T.tj, h), hc(T.ti, h), (2048.0, 6144.0)[t % 2], None, ALU.add, None, [K("ti", h)], [K("tj", h)])
        cut = lambda h: ts(hc(T.ta, h), hc(T.tj, h), 1, 4095, ALU.arith_shift_right, ALU.bitwise_and, [K("tj", h)], [K("ta", h)])

        def move(h):
            ts(hc(T.zh, h), hc(T.ta, h), -2048.0, None, ALU.add, None, [K("ta", h)], [K("zh", h)])
            ev, od = T.zh[:, 128 * h:128 * h + 128:2], T.zh[:, 128 * h + 1:128 * h + 128:2]
            bk = 4 + h
            mm(bk, ps[bk][:, 128:192], mat("DL"), ev, True, False, ["DL", K("zh", h)])
            mm(bk, ps[bk][:, 128:192], mat("UP"), od, False, True, ["UP", K("zh", h)])
            mm(bk, ps[bk][:, 192:256], mat("DN"), ev, True, False, ["DN", K("zh", h)])
            mm(bk, ps[bk][:, 192:256], mat("DH"), od, False, True, ["DH", K("zh", h)])

        def word(h):
            if not last:
                mm(6 + h, ps[6 + h][:, 384:512], I, hc(T.xh, h), True, False, ["I", K("xh", h)])
                mm(6 + h, ps[6 + h][:, 384:512], T.qy[:], hc(T.kg, h), False, True, ["qy", "kg"])
                a = BLK * (t + 2) + LANES * rank + 128 * h
                act(T.ew[:, a:a + 128], ps[6 + h][:, 384:512], ACT.Identity, [], [K("word", h)], (6 + h,), bias=-float(2 ** 23))

        lists = lambda h: ts(hc(T.ll, h), ps[4 + h][:, 128:256], 2048.0, None, ALU.add, None, [], [K("ll", h)], (4 + h,))
        again = lambda bk: None if last else floor_of(bk)
        nb = "nb%d" % (t % 2)

        def bind(h):
            mm(6 + h, ps[6 + h][:, 0:128], mat("SH"), hc(T.xh, h), True, False, ["SH", K("xh", h)])
            mm(6 + h, ps[6 + h][:, 0:128], D0, hc(T.nt, h), False, False, ["zrow", "nt"])
            mm(6 + h, ps[6 + h][:, 0:128], D0, T[nb][:], False, False, ["zrow", nb])
            mm(6 + h, ps[6 + h][:, 0:128], T.qk[:], hc(T.kg, h), False, True, ["qk", "kg"])

        def clear(h):
            mm(4 + h, ps[4 + h][:, 0:128], mat("ON"), T.csum[:], True, False, ["ON", "csum"])
            mm(6 + h, ps[6 + h][:, 128:256], I, hc(T.zg, h), True, False, ["I", "zg"])

        def spread(_):
            for s in range(16):
                mm(3, ps[3][:, 0:16], T.zrow[:, 16 - s:144 - s], T.zh[:, s:256:16], s == 0, s == 15, ["zrow", "zhA", "zhB"])

        run(((pick, 0), (pick, 1), (half, 0), (word, 0), (again, 0), (again, 1), (bind, 0), (pick, 2), (turn, 0), (pick, 3), (again, 2), (cut, 0),
             (half, 1), (word, 1), (move, 0), (turn, 1), (lists, 0), (bind, 1), (cut, 1), (move, 1), (clear, 0), (spread, 0)))
        if not last:
            both("own_e%d" % (t + 2), "wordA", "wordB")

        have = [xin[t], xin[t + 1], "own_x%d" % t, "own_x%d" % (t + 1)]
        if not last:
            send("me%d" % t, have + ["own_e%d" % (t + 2)])
        win = T.xw[:, BLK * t:BLK * (t + 2)]
        wap = T.w4[:] if last else _piece(T, "mw%d" % t, rank)
        wbuf, w0 = (T.w4, 0) if last else (T.xw, BLK * (t + 2) + LANES * rank)
        wh = lambda h: wbuf[:, w0 + 128 * h:w0 + 128 * h + 128]
        wk = "own_x%d" % (t + 2)

        def upper(c):
            a, h, o = 256 * c, c // 4, 128 * (c // 4) + 16 * (c % 4)
            act(T.ga[:, a:a + 256], win.indirect(T.ll[:, o + 64:o + 80]), ACT.Copy, have + [K("ll", h)], ["ga%d" % c])

        def lower(c):
            a, h, o = 256 * c, c // 4, 128 * (c // 4) + 16 * (c % 4)
            tt(T.mx[:, a:a + 256], win.indirect(T.ll[:, o:o + 16]), T.ga[:, a:a + 256], ALU.max,
               have + [K("ll", h), "ga%d" % c], ["mx%d" % c])

        def add(q, bk, o):
            for k in range(8):
                mm(bk, ps[bk][:, o:o + 64], I, T.mx[:, 512 * q + k:512 * q + 512:8], False,
                   bk < 6 and q % 2 == 1 and k == 7, ["I", "mx%d" % (2 * q), "mx%d" % (2 * q + 1)])

        sums = lambda q: add(q, 4 + q // 2, 64 * (q % 2))
        less = lambda q: add(q, 6 + q // 2, 128 + 64 * (q % 2))

        first = lambda _: ts(T.l0[:], ps[3][:, 0:16], 2048.0, None, ALU.add, None, [], ["l0"], (3,))
        closure = lambda h: act(hc(T.aw, h), T.ew[:, BLK * t:BLK * (t + 2)].indirect(h8(T.l0, h)), ACT.Copy,
                                [ein[t], ein[t + 1], "own_e%d" % t, "own_e%d" % (t + 1), "l0"], [K("aw", h)])
        rest = lambda h: act(hc(T.xr, h), ps[4 + h][:, 0:128], ACT.Identity, [], [K("xr", h)], (4 + h,), scale=-1.0, bias=127.5)
        value = lambda h: tt(wh(h), ps[4 + h][:, 0:128], hc(T.xr, h), ALU.add, [K("xr", h)], [K(wk, h)], (4 + h,))
        margin = lambda h: mm(6 + h, ps[6 + h][:, 128:256], I, hc(T.xr, h), False, True, ["I", K("xr", h)])
        reach = lambda h: act(hc(T.yes, h), ps[6 + h][:, 128:256], ACT.Sign, [], [K("yes", h)], (6 + h,), bias=49152.5)

        def vote(h):
            mm(6 + h, ps[6 + h][:, 256:384], mat("ON"), T.cvote[:], True, False, ["ON", "cvote"])
            mm(6 + h, ps[6 + h][:, 256:384], mat("ON"), hc(T.yes, h), False, True, ["ON", K("yes", h)])

        def leave(_):
            both(wk, K(wk, 0), K(wk, 1))
            if not last:
                send("mw%d" % t, [wk])
            deps("y", [wk], (), ())
            g.sync.dma_start(T.yx[:, 256 * t:256 * (t + 1)], wap).then_inc(T.sem.sto, 16)

        low = lambda h: tt(hc(T.v2, h), ps[6 + h][:, 256:384], hc(T.aw, h), ALU.max, [K("aw", h)], [K("v2", h)], (6 + h,))
        high = lambda h: tt(hc(T.pw, h), ps[6 + h][:, 0:128], hc(T.v2, h), ALU.min, [K("v2", h)], [K("pw", h)], (6 + h,))
        if t == 0:
            twice(0)
        run(((upper, 0), (lower, 0), (lists, 1), (clear, 1)))
        for c in range(1, 8):
            upper(c)
        run(((lower, 1), (first, 0), (sums, 0), (less, 0), (again, 3), (lower, 2), (lower, 3), (sums, 1), (less, 1), (lower, 4), (lower, 5),
             (sums, 2), (rest, 0), (margin, 0), (less, 2), (lower, 6), (lower, 7), (sums, 3), (value, 0)))
        if last:
            run(((closure, 0), (reach, 0), (vote, 0), (less, 3), (low, 0), (rest, 1), (margin, 1), (closure, 1), (reach, 1), (vote, 1)))
        else:
            run(((reach, 0), (vote, 0), (less, 3), (rest, 1), (margin, 1), (value, 1), (leave, 0), (closure, 0), (low, 0), (reach, 1), (vote, 1), (closure, 1)))
        nsto += 16
        if not last:
            run(((high, 0), (round1, 0), (diag, 0), (low, 1), (code, 0), (high, 1), (round2, 0), (pair, 0), (round1, 1), (diag, 1), (name, 0),
                 (code, 1), (round2, 1), (pair, 1), (name, 1)))

    whole = lambda h: ts(hc(T.ti, h), hc(T.pw, h), 2.0 ** -13, None, ALU.mult, None, [K("pw", h)], [K("ti", h)])
    mask = lambda h: ts(hc(T.ta, h), hc(T.ti, h), 1023, None, ALU.bitwise_and, None, [K("ti", h)], [K("ta", h)])
    plain = lambda h: tt(hc(T.xf, h), hc(T.pw, h), ps[4 + h][:, 384:512], ALU.subtract, [K("pw", h)], [K("xf", h)], (4 + h,))
    block = lambda h: ts(hc(T.bb, h), hc(T.xf, h), 0.0, -3840.0, ALU.is_ge, ALU.mult, [K("xf", h)], [K("bb", h)])
    piece = lambda h: act(hc(T.hb, h), hc(T.xf, h), ACT.Identity, [K("xf", h)], [K("hb", h)], bias=49152 - 127.5)

    def names(h):
        mm(h, ps[h][:, 0:128], T.idf[:], hc(T.xf, h), True, False, ["idf", K("xf", h)])
        mm(h, ps[h][:, 0:128], I, hc(T.bb, h), False, False, ["I", K("bb", h)])
        mm(h, ps[h][:, 0:128], I, hc(T.hb, h), False, True, ["I", K("hb", h)])

    def store(h):
        ts(hc(T.oe, h), ps[h][:, 0:128], 4096.0 - 49152.0, None, ALU.add, None, [], [K("oe", h)], (h,))
        q = "ys"[h]
        deps(q, [K("oe", h)], (), ())
        Q[q].dma_start(T.ye[:, 128 * h:128 * h + 128], hc(T.oe, h)).then_inc(T.sem.sto, 16)

    def codes(_):
        cp(T.oc[:], T.ta[:], ["taA", "taB"], ["oc"])
        deps("y", ["oc"], (), ())
        g.sync.dma_start(T.yc[:], T.oc[0:128:16, :]).then_inc(T.sem.sto, 16)

    run(((high, 0), (round1, 0), (value, 1), (leave, 0), (low, 1), (round2, 0), (high, 1), (round1, 1), (plain, 0), (round2, 1), (block, 0),
         (piece, 0), (names, 0), (whole, 0), (plain, 1), (piece, 1), (block, 1), (names, 1), (whole, 1), (mask, 0), (mask, 1), (store, 0),
         (store, 1), (codes, 0)))
    nsto += 48
    for q in "vspg":
        g.wait_ge(T.sem["s" + q], count[q])
    g.wait_ge(T.sem.sent, sent[0])
    g.wait_ge(T.sem.sto, nsto)
